import numpy as np
import ml_dtypes


def mxq(x, axis, fmt="e4m3"):
    dtype, down = {"e4m3": (ml_dtypes.float8_e4m3fn, 7), "e5m2": (ml_dtypes.float8_e5m2, 14)}[fmt]
    v = np.moveaxis(np.asarray(x, np.float32).astype(ml_dtypes.bfloat16).astype(np.float64), axis, -1)
    blocks = v.reshape(v.shape[:-1] + (-1, 32))
    amax = np.abs(blocks).max(-1, keepdims=True)
    byte = np.maximum(np.where(amax > 0, np.frexp(amax)[1] - 1 + 127, 0) - down, 1)
    scale = np.exp2(byte - 127.0)
    codes = (blocks / scale).astype(np.float32).astype(dtype).astype(np.float64)
    return np.moveaxis((codes * scale).reshape(v.shape), -1, axis)


WIDE = False


def mx_kscale(k):
    if not WIDE:
        return np.ones(k)
    levels = np.array([24, -24, 12, -12, 0])
    if k % 512:
        return np.exp2(np.random.permutation(np.resize(levels, k // 32))).repeat(32)
    a = np.empty((k // 512, 16))
    for p in range(k // 512):
        a[p, :8] = np.random.permutation(np.resize(levels, 8))
        for g in range(8):
            far = levels[np.abs(levels - a[p, g]) >= 10]
            a[p, g + 8] = far[np.random.randint(len(far))]
    return np.exp2(a.ravel()).repeat(32)


def f64(x):
    return np.asarray(x).astype(np.float64)


def striped(idx):
    return np.tile(idx.reshape(-1, 16).T, (8, 1)).astype(np.uint16)


def unstriped(offs):
    return offs[:16].T.reshape(-1).astype(np.int64)


E2M1 = np.array([0.0, 0.5, 1.0, 1.5, 2.0, 3.0, 4.0, 6.0, -0.0, -0.5, -1.0, -1.5, -2.0, -3.0, -4.0, -6.0])


def pack_weight(w, fmt):
    k, n = w.shape
    w = f64(np.asarray(w, np.float32).astype(ml_dtypes.bfloat16)).reshape(k // 32, 32, n)
    amax = np.abs(w).max(1)
    if fmt == "e4m3":
        byte = np.frexp(amax)[1] - 1 + 127 - 7
    else:
        mant, ex = np.frexp(amax / 6.0)
        byte = np.where(mant > 0.5, ex, ex - 1) + 127
    byte = np.clip(np.where(amax > 0, byte, 1), 1, 254)
    scaled = (w * np.exp2(127.0 - byte)[:, None, :]).reshape(k, n).astype(np.float32)
    by_word = np.ascontiguousarray(scaled.reshape(k // 512, 128, 4, n).transpose(0, 1, 3, 2))
    if fmt == "e4m3":
        words = by_word.astype(ml_dtypes.float8_e4m3fn).view(np.uint8)
    else:
        c = by_word.astype(ml_dtypes.float4_e2m1fn).view(np.uint8) & 0xF
        words = (c[..., 0::2] | (c[..., 1::2] << 4)).reshape(k // 512, 128, 2 * n)
    return np.ascontiguousarray(words), np.ascontiguousarray(byte.astype(np.uint8).reshape(k // 512, 16, n))


def unpack_weight(words, scales, fmt):
    g, _, n = scales.shape
    words = np.ascontiguousarray(words).reshape(g, 128, n, -1)
    if fmt == "e4m3":
        vals = words.view(ml_dtypes.float8_e4m3fn).astype(np.float64)
    else:
        nib = np.empty((g, 128, n, 4), np.uint8)
        nib[..., 0::2] = words & 0xF
        nib[..., 1::2] = words >> 4
        vals = E2M1[nib]
    vals = vals * np.repeat(np.exp2(scales.astype(np.float64) - 127.0), 8, axis=1)[..., None]
    return vals.transpose(0, 1, 3, 2).reshape(g * 512, n)


def planes(y):
    n, m = y.shape
    v = y.astype(np.float32).astype(ml_dtypes.bfloat16).astype(np.float64).reshape(n // 32, 32, m)
    top = np.abs(v).max(1)
    byte = np.clip(np.where(top > 0, np.frexp(top)[1] - 1 + 127 - 7, 1), 1, 254)
    codes = (v * np.exp2(127.0 - byte)[:, None, :]).reshape(n, m).astype(np.float32).astype(ml_dtypes.float8_e4m3fn).view(np.uint8)
    words = codes.reshape(n // 512, 128, 4, m).transpose(0, 1, 3, 2)
    return np.ascontiguousarray(words), np.ascontiguousarray(byte.astype(np.uint8).reshape(n // 512, 16, m))


def sigm(f):
    return 1.0 / (1.0 + np.exp(-np.maximum(f, -700.0)))


K, N, T, J = 1024, 512, 2048, 1024


def setup_inputs():
    n = np.random.standard_normal
    s = mx_kscale(K)[:, None]
    p_tab = pack_weight(n((K, T)) * s, "e4m3")
    p_wb = pack_weight(n((K, N)) / np.sqrt(2 * K) / s, "e2m1")
    p_wc = pack_weight(n((K, N)) / np.sqrt(K) / s, "e4m3")
    return {
        "tab_words": p_tab[0],
        "tab_scales": p_tab[1],
        "wa": (n((K, N)) / np.sqrt(2 * K) / s).astype(np.float32),
        "wb_words": p_wb[0],
        "wb_scales": p_wb[1],
        "wc_words": p_wc[0],
        "wc_scales": p_wc[1],
        "wo": (n((K, N)) / np.sqrt(K) / s).astype(np.float32),
        "wgo": np.tile(np.random.uniform(0.5, 2.0, J), (128, 1)).astype(np.float32),
        "offs": striped(np.random.permutation(T)[:J]),
        "offs2": striped(np.random.permutation(T)[:J]),
    }


def reference(tab_words, tab_scales, wa, wb_words, wb_scales, wc_words, wc_scales, wo, wgo, offs, offs2):
    idx = unstriped(offs)
    idx2 = unstriped(offs2)
    tab_ = unpack_weight(tab_words, tab_scales, "e4m3")[:, idx]
    tabb_ = unpack_weight(tab_words, tab_scales, "e4m3")[:, idx2]
    wa_ = mxq(f64(wa), 0, "e4m3")
    wb_ = unpack_weight(wb_words, wb_scales, "e2m1")
    za = wa_.T @ tabb_ + wb_.T @ tab_
    eta = sigm(za)
    wc_ = unpack_weight(wc_words, wc_scales, "e4m3")
    ms = wc_.T @ tab_
    wo_ = mxq(f64(wo), 0, "e4m3")
    ow = wo_.T @ tabb_
    out = np.zeros((N, T))
    out[:, idx2] = f64(wgo)[0] * (ow + eta * ms)
    return (out,) + planes(out)

@@ -1,0 +1,291 @@
+from contextlib import ExitStack
+
+import concourse.mybir as mybir
+from concourse.masks import make_identity
+
+K, N, T, J = 1024, 512, 2048, 1024
+FLOPS = 2 * 4 * K * N * J
+
+F32 = mybir.dt.float32
+BF16 = mybir.dt.bfloat16
+I32 = mybir.dt.int32
+U32 = mybir.dt.uint32
+U16 = mybir.dt.uint16
+U8 = mybir.dt.uint8
+FP8X4 = mybir.dt.float8_e4m3fn_x4
+FP4X4 = mybir.dt.float4_e2m1fn_x4
+MULT = mybir.AluOpType.mult
+ACT = mybir.ActivationFunctionType
+
+P = 128
+PACK = 4
+PASSES = K // (P * PACK)
+HALF = 512
+TILES = HALF // P
+CHUNK = 512
+CHUNKS = T // CHUNK
+QUADS = 4
+SHIFT_ROWS = 100
+
+
+def tile_list_rgg_ownP_kernel(
+    tc, tab_words, tab_scales, wa, wb_words, wb_scales, wc_words, wc_scales, wo, wgo, offs, offs2, out_0, out_1, out_2
+):
+    nc = tc.nc
+    with ExitStack() as ctx:
+        lists = ctx.enter_context(tc.tile_pool(name="lists", bufs=1))
+        keep = ctx.enter_context(tc.tile_pool(name="keep", bufs=1))
+        psum = ctx.enter_context(tc.psum_pool(name="psum", bufs=1))
+
+        def sb(name, shape, dtype, tag=None):
+            return keep.tile(shape, dtype, name=name, tag=tag or name, align_bytes=64)
+
+        def bank(b, name):
+            return psum.tile([P, N], F32, name=name, tag="bank%d" % b)
+
+        src_list = lists.tile([P, J // 16], U16, name="src_list")
+        dst_list = lists.tile([P, J // 16], U16, name="dst_list")
+        nc.sync.dma_start(src_list[:], offs)
+        nc.sync.dma_start(dst_list[:], offs2)
+        both_lists = (src_list, dst_list)
+
+        def half_list(lst, h):
+            return lst[:, h * HALF // 16 : (h + 1) * HALF // 16]
+
+        warm = sb("warm", [P, 1], F32)
+        nc.vector.memset(warm[:], 0.0)
+        warm_out = sb("warm_out", [P, 1], F32)
+        nc.scalar.activation(warm_out[:], warm[:], ACT.Sigmoid)
+
+        tab_s = sb("tab_s", [P, T], U8)
+        nc.vector.memset(tab_s[:].bitcast(I32), 0)
+        for q in range(QUADS):
+            nc.sync.dma_start(tab_s[32 * q : 32 * q + 8, :].bitcast(I32), tab_scales[:, 4 * q : 4 * q + 4, :].bitcast(I32))
+
+        wb_s = sb("wb_s", [P, PASSES, N], U8)
+        wc_s = sb("wc_s", [P, PASSES, N], U8)
+        gate_rows = sb("gate_rows", [P, P], F32)
+        src_s1 = sb("src_s1", [P, J], U8)
+        nc.vector.memset(wb_s[:].bitcast(I32), 0)
+        nc.vector.memset(wc_s[:].bitcast(I32), 0)
+        nc.vector.memset(gate_rows[:], 0.0)
+        nc.vector.memset(src_s1[:].bitcast(I32), 0)
+        for plane, scales in ((wb_s, wb_scales), (wc_s, wc_scales)):
+            for q in range(QUADS):
+                nc.gpsimd.dma_start(
+                    plane[32 * q : 32 * q + 4, :, :].bitcast(I32),
+                    scales[:, 4 * q : 4 * q + 4, :].rearrange("a r n -> r a n").bitcast(I32),
+                )
+        nc.gpsimd.dma_start(gate_rows[0 : J // P, :], wgo[0:1, :].rearrange("o (b c) -> (o b) c", c=P))
+        ident = sb("ident", [P, P], F32)
+        make_identity(nc, ident[:])
+
+        def load_rows(w, a, name):
+            raw = sb(name, [P, PACK, N], F32)
+            nc.sync.dma_start(raw[:], w[a * P * PACK : (a + 1) * P * PACK, :].rearrange("(p i) n -> p i n", i=PACK))
+            return raw
+
+        def load_table(a):
+            words = sb("tab_w%d" % a, [P, T], I32)
+            nc.sync.dma_start(words[:], tab_words[a].rearrange("p t i -> p (t i)").bitcast(I32))
+            return words
+
+        wa_raw, wo_raw, tab_w = [], [], []
+        for a in range(PASSES):
+            wa_raw.append(load_rows(wa, a, "wa_raw%d" % a))
+            tab_w.append(load_table(a))
+        for a in range(PASSES):
+            wo_raw.append(load_rows(wo, a, "wo_raw%d" % a))
+        wb_w = sb("wb_w", [P, PASSES, 2 * N], U8)
+        nc.sync.dma_start(wb_w[:].bitcast(I32), wb_words.rearrange("a p b -> p a b").bitcast(I32))
+        wc_w = sb("wc_w", [P, PASSES, N], U32)
+        nc.sync.dma_start(wc_w[:].bitcast(I32), wc_words.rearrange("a p n i -> p a (n i)").bitcast(I32))
+
+        src_s = sb("src_s", [P, J], U8)
+        dst_s = sb("dst_s", [P, J], U8)
+        nc.vector.tensor_copy(src_s[:], tab_s[:].indirect(src_list[:]))
+        nc.scalar.dma_start(src_s1[0:SHIFT_ROWS, :].bitcast(I32), src_s[4 : 4 + SHIFT_ROWS, :].bitcast(I32))
+        nc.vector.tensor_copy(dst_s[:], tab_s[:].indirect(dst_list[:]))
+
+        gate_ps = bank(7, "gate_ps")
+        nc.tensor.transpose(gate_ps[:, 0:P], gate_rows[:], ident[:])
+        gate = sb("gate", [P, J // P], F32)
+        nc.scalar.copy(gate[:], gate_ps[:, 0 : J // P])
+
+        pages = []
+        for t in range(PACK):
+            page = sb("page%d" % t, [P, T], F32)
+            nc.vector.memset(page[:].bitcast(I32), 0)
+            pages.append(page)
+
+        def gather_words(h, a, tag=None):
+            picked = sb("picked%d%d" % (h, a), [P, 2, HALF], U32, tag)
+            for s in range(2):
+                nc.vector.tensor_copy(picked[:, s, :], tab_w[a][:].bitcast(U32).indirect(half_list(both_lists[s], h)))
+            return picked
+
+        def quantise_weight(raw, name):
+            grouped = sb(name + "_bf", [P, N, PACK], BF16, name + "_slot")
+            nc.scalar.copy(
+                grouped[:].rearrange("p (c e) i -> p c i e", e=4), raw[:].rearrange("p i (c e) -> p c i e", e=4)
+            )
+            codes = sb(name + "_codes", [P, N], U32)
+            scales = sb(name + "_scales", [P, N], U8)
+            nc.vector.quantize_mx(out=codes[:].bitcast(FP8X4), scales=scales[:], in_=grouped[:].rearrange("p n i -> p (n i)"))
+            return codes[:].bitcast(FP8X4), scales[:]
+
+        picked = {}
+        picked[0, 0] = gather_words(0, 0)
+        wa_q = [quantise_weight(wa_raw[0], "wa0")]
+        picked[0, 1] = gather_words(0, 1)
+        wa_q.append(quantise_weight(wa_raw[1], "wa1"))
+        picked[1, 0] = gather_words(1, 0, "wa1_slot")
+        wo_q = [quantise_weight(wo_raw[0], "wo0")]
+        picked[1, 1] = gather_words(1, 1, "wo0_slot")
+        wo_q.append(quantise_weight(wo_raw[1], "wo1"))
+        wb_q = [(wb_w[:, a, :].bitcast(FP4X4), wb_s[:, a, :]) for a in range(PASSES)]
+        wc_q = [(wc_w[:, a, :].bitcast(FP8X4), wc_s[:, a, :]) for a in range(PASSES)]
+
+        def mx_pass(acc, h, jt, s, a, weight, start, stop):
+            cols = slice(h * HALF + jt * P, h * HALF + (jt + 1) * P)
+            if s == 0:
+                plane = (src_s, src_s1)[a][:, cols]
+            else:
+                plane = dst_s[4 * a : P, cols]
+            nc.tensor.matmul_mx(
+                out=acc[:],
+                lhsT=picked[h, a][:, s, jt * P : (jt + 1) * P].bitcast(FP8X4),
+                lhsT_scale=plane,
+                rhs=weight[a][0],
+                rhs_scale=weight[a][1],
+                start=start,
+                stop=stop,
+            )
+
+        def dealt(acc):
+            return acc[:].rearrange("p (m t) -> p t m", t=PACK)
+
+        def sigmoid(acc, name, jt):
+            eta = sb(name, [P, PACK, P], F32, "eta%d" % jt)
+            nc.scalar.activation(eta[:], dealt(acc), ACT.Sigmoid)
+            return eta
+
+        def gate_col(h, jt):
+            return gate[:, h * TILES + jt : h * TILES + jt + 1]
+
+        def message(dst, acc, eta, h, jt):
+            nc.vector.scalar_tensor_tensor(dst[:, jt], dealt(acc), gate_col(h, jt), eta[:], MULT, MULT)
+
+        def own(dst, acc, h, jt):
+            nc.scalar.activation(dst[:, jt], dealt(acc), ACT.Copy, scale=gate_col(h, jt))
+
+        def turn(b, h, t, msg, ow, tag=None):
+            acc = bank(b, "turn%d%d" % (h, t))
+            for jt in range(TILES):
+                cols = acc[:, jt * P : (jt + 1) * P]
+                nc.tensor.matmul(cols, ow[:, jt, t, :], ident[:], start=True, stop=False, is_transpose=True)
+                nc.tensor.matmul(cols, msg[:, jt, t, :], ident[:], start=False, stop=True, is_transpose=True)
+            vals = sb("vals%d%d" % (h, t), [P, HALF], F32, tag)
+            nc.scalar.copy(vals[:], acc[:])
+            return vals
+
+        def scatter(h, t, vals):
+            nc.vector.tensor_copy(pages[t][:].indirect(half_list(dst_list, h)), vals[:])
+
+        za = [bank(jt, "za0%d" % jt) for jt in range(TILES)]
+        for a in range(PASSES):
+            for jt in range(TILES):
+                mx_pass(za[jt], 0, jt, 1, a, wa_q, a == 0, False)
+        eta = []
+        for jt in range(TILES):
+            for a in range(PASSES):
+                mx_pass(za[jt], 0, jt, 0, a, wb_q, False, a == PASSES - 1)
+            eta.append(sigmoid(za[jt], "eta0%d" % jt, jt))
+        ms = [bank(jt, "ms0%d" % jt) for jt in range(TILES)]
+        msg0 = sb("msg0", [P, TILES, PACK, P], F32, "wo1_slot")
+        for jt in range(TILES):
+            for a in range(PASSES):
+                mx_pass(ms[jt], 0, jt, 0, a, wc_q, a == 0, a == PASSES - 1)
+            message(msg0, ms[jt], eta[jt], 0, jt)
+        ow = [bank(TILES + jt, "ow0%d" % jt) for jt in range(TILES)]
+        own0 = sb("own0", [P, TILES, PACK, P], F32)
+        for jt in range(TILES):
+            mx_pass(ow[jt], 0, jt, 1, 0, wo_q, True, False)
+        for jt in range(TILES):
+            mx_pass(ow[jt], 0, jt, 1, 1, wo_q, False, True)
+            own(own0, ow[jt], 0, jt)
+
+        order = (2, 0, 1, 3)
+        for b in range(3):
+            scatter(0, order[b], turn(b, 0, order[b], msg0, own0))
+
+        eta = []
+        for jt in range(TILES):
+            acc = bank(3 + jt, "za1%d" % jt)
+            for a in range(PASSES):
+                mx_pass(acc, 1, jt, 1, a, wa_q, a == 0, False)
+            for a in range(PASSES):
+                mx_pass(acc, 1, jt, 0, a, wb_q, False, a == PASSES - 1)
+            eta.append(sigmoid(acc, "eta1%d" % jt, jt))
+        own1 = sb("own1", [P, TILES, PACK, P], F32)
+        for jt in range(TILES):
+            acc = bank((7, 3, 4, 5)[jt], "ow1%d" % jt)
+            for a in range(PASSES):
+                mx_pass(acc, 1, jt, 1, a, wo_q, a == 0, a == PASSES - 1)
+            own(own1, acc, 1, jt)
+        msg1 = sb("msg1", [P, TILES, PACK, P], F32)
+        for jt in range(TILES):
+            acc = bank((0, 1, 2, 6)[jt], "ms1%d" % jt)
+            for a in range(PASSES):
+                mx_pass(acc, 1, jt, 0, a, wc_q, a == 0, a == PASSES - 1)
+            message(msg1, acc, eta[jt], 1, jt)
+
+        pairs = [sb("pairs%d" % c, [P, 2, CHUNK, 2], BF16) for c in range(CHUNKS)]
+        out_rows = out_0.rearrange("(p t) c -> p t c", t=PACK)
+
+        def round_page(t, c, copy):
+            copy(pairs[c][:, t // 2, :, t % 2], pages[t][:, c * CHUNK : (c + 1) * CHUNK])
+
+        def finish_page(t):
+            nc.sync.dma_start(out_rows[:, t, :], pages[t][:])
+            for c in range(CHUNKS):
+                round_page(t, c, nc.scalar.copy)
+
+        scatter(0, order[3], turn(0, 0, order[3], msg0, own0))
+        scatter(1, order[0], turn(7, 1, order[0], msg1, own1, "vals_last"))
+        vals_b = turn(3, 1, order[1], msg1, own1)
+        vals_c = turn(4, 1, order[2], msg1, own1)
+        finish_page(order[0])
+        scatter(1, order[1], vals_b)
+        vals_d = turn(5, 1, order[3], msg1, own1, "vals_last")
+        finish_page(order[1])
+        scatter(1, order[2], vals_c)
+        finish_page(order[2])
+        scatter(1, order[3], vals_d)
+
+        last = order[3]
+        nc.sync.dma_start(out_rows[:, last, :], pages[last][:])
+        woven = [sb("woven%d" % c, [P, CHUNK, 2, 2], BF16) for c in range(CHUNKS)]
+
+        def weave(c, copy):
+            copy(woven[c][:], pairs[c][:].rearrange("p u c e -> p c u e"))
+
+        for c in (2, 3):
+            round_page(last, c, nc.scalar.copy)
+            weave(c, nc.scalar.copy)
+        for c in (0, 1):
+            round_page(last, c, nc.vector.tensor_copy)
+        for c in (0, 1):
+            weave(c, nc.vector.tensor_copy)
+        out_s = sb("out_s", [P, T], U8)
+        out_words = out_1[0].rearrange("p t i -> p (t i)").bitcast(I32)
+        for c in range(CHUNKS):
+            cols = slice(c * CHUNK, (c + 1) * CHUNK)
+            codes = sb("out_w%d" % c, [P, CHUNK], U32)
+            nc.vector.quantize_mx(
+                out=codes[:].bitcast(FP8X4), scales=out_s[:, cols], in_=woven[c][:].rearrange("p c u e -> p (c u e)")
+            )
+            nc.sync.dma_start(out_words[:, cols], codes[:].bitcast(I32))
+        for q in range(QUADS):
+            queue = (nc.scalar, nc.sync)[q % 2]
+            queue.dma_start(out_2[0, 4 * q : 4 * q + 4, :].bitcast(I32), out_s[32 * q : 32 * q + 4, :].bitcast(I32))

@@ -52,33 +52,27 @@ def tile_list_rgg_ownP_kernel(
         def half_list(lst, h):
             return lst[:, h * HALF // 16 : (h + 1) * HALF // 16]
 
-        warm = sb("warm", [P, 1], F32)
-        nc.vector.memset(warm[:], 0.0)
-        warm_out = sb("warm_out", [P, 1], F32)
-        nc.scalar.activation(warm_out[:], warm[:], ACT.Sigmoid)
-
         tab_s = sb("tab_s", [P, T], U8)
-        nc.vector.memset(tab_s[:].bitcast(I32), 0)
+        gate_rows = sb("gate_rows", [P, P], F32)
+        ident = sb("ident", [P, P], F32)
+        nc.gpsimd.memset(tab_s[:].bitcast(I32), 0)
+        nc.gpsimd.memset(gate_rows[:], 0.0)
+        make_identity(nc, ident[:])
+        wb_s = sb("wb_s", [P, PASSES, N], U8)
+        wc_s = sb("wc_s", [P, PASSES, N], U8)
+        src_s1 = sb("src_s1", [P, J], U8)
+        for plane in (wb_s, wc_s, src_s1):
+            nc.vector.memset(plane[:].bitcast(I32), 0)
+
         for q in range(QUADS):
             nc.sync.dma_start(tab_s[32 * q : 32 * q + 8, :].bitcast(I32), tab_scales[:, 4 * q : 4 * q + 4, :].bitcast(I32))
 
-        wb_s = sb("wb_s", [P, PASSES, N], U8)
-        wc_s = sb("wc_s", [P, PASSES, N], U8)
-        gate_rows = sb("gate_rows", [P, P], F32)
-        src_s1 = sb("src_s1", [P, J], U8)
-        nc.vector.memset(wb_s[:].bitcast(I32), 0)
-        nc.vector.memset(wc_s[:].bitcast(I32), 0)
-        nc.vector.memset(gate_rows[:], 0.0)
-        nc.vector.memset(src_s1[:].bitcast(I32), 0)
-        for plane, scales in ((wb_s, wb_scales), (wc_s, wc_scales)):
+        def load_scales(plane, scales):
             for q in range(QUADS):
-                nc.gpsimd.dma_start(
+                nc.sync.dma_start(
                     plane[32 * q : 32 * q + 4, :, :].bitcast(I32),
                     scales[:, 4 * q : 4 * q + 4, :].rearrange("a r n -> r a n").bitcast(I32),
                 )
-        nc.gpsimd.dma_start(gate_rows[0 : J // P, :], wgo[0:1, :].rearrange("o (b c) -> (o b) c", c=P))
-        ident = sb("ident", [P, P], F32)
-        make_identity(nc, ident[:])
 
         def load_rows(w, a, name):
             raw = sb(name, [P, PACK, N], F32)
@@ -91,20 +85,24 @@ def tile_list_rgg_ownP_kernel(
             return words
 
         wa_raw, wo_raw, tab_w = [], [], []
-        for a in range(PASSES):
-            wa_raw.append(load_rows(wa, a, "wa_raw%d" % a))
-            tab_w.append(load_table(a))
+        wa_raw.append(load_rows(wa, 0, "wa_raw0"))
+        tab_w.append(load_table(0))
+        nc.sync.dma_start(gate_rows[0 : J // P, :], wgo[0:1, :].rearrange("o (b c) -> (o b) c", c=P))
+        wa_raw.append(load_rows(wa, 1, "wa_raw1"))
+        tab_w.append(load_table(1))
+        load_scales(wb_s, wb_scales)
         for a in range(PASSES):
             wo_raw.append(load_rows(wo, a, "wo_raw%d" % a))
         wb_w = sb("wb_w", [P, PASSES, 2 * N], U8)
         nc.sync.dma_start(wb_w[:].bitcast(I32), wb_words.rearrange("a p b -> p a b").bitcast(I32))
         wc_w = sb("wc_w", [P, PASSES, N], U32)
         nc.sync.dma_start(wc_w[:].bitcast(I32), wc_words.rearrange("a p n i -> p a (n i)").bitcast(I32))
+        load_scales(wc_s, wc_scales)
 
         src_s = sb("src_s", [P, J], U8)
         dst_s = sb("dst_s", [P, J], U8)
         nc.vector.tensor_copy(src_s[:], tab_s[:].indirect(src_list[:]))
-        nc.scalar.dma_start(src_s1[0:SHIFT_ROWS, :].bitcast(I32), src_s[4 : 4 + SHIFT_ROWS, :].bitcast(I32))
+        nc.sync.dma_start(src_s1[0:SHIFT_ROWS, :].bitcast(I32), src_s[4 : 4 + SHIFT_ROWS, :].bitcast(I32))
         nc.vector.tensor_copy(dst_s[:], tab_s[:].indirect(dst_list[:]))
 
         gate_ps = bank(7, "gate_ps")
@@ -112,11 +110,15 @@ def tile_list_rgg_ownP_kernel(
         gate = sb("gate", [P, J // P], F32)
         nc.scalar.copy(gate[:], gate_ps[:, 0 : J // P])
 
-        pages = []
-        for t in range(PACK):
-            page = sb("page%d" % t, [P, T], F32)
-            nc.vector.memset(page[:].bitcast(I32), 0)
-            pages.append(page)
+        order = (2, 0, 1, 3)
+        pages = {}
+
+        def clear_page(t, tag=None):
+            pages[t] = sb("page%d" % t, [P, T], F32, tag)
+            nc.vector.memset(pages[t][:].bitcast(I32), 0)
+
+        for t in order[:3]:
+            clear_page(t)
 
         def gather_words(h, a, tag=None):
             picked = sb("picked%d%d" % (h, a), [P, 2, HALF], U32, tag)
@@ -141,8 +143,8 @@ def tile_list_rgg_ownP_kernel(
         wa_q.append(quantise_weight(wa_raw[1], "wa1"))
         picked[1, 0] = gather_words(1, 0, "wa1_slot")
         wo_q = [quantise_weight(wo_raw[0], "wo0")]
-        picked[1, 1] = gather_words(1, 1, "wo0_slot")
         wo_q.append(quantise_weight(wo_raw[1], "wo1"))
+        clear_page(order[3], "wo1_slot")
         wb_q = [(wb_w[:, a, :].bitcast(FP4X4), wb_s[:, a, :]) for a in range(PASSES)]
         wc_q = [(wc_w[:, a, :].bitcast(FP8X4), wc_s[:, a, :]) for a in range(PASSES)]
 
@@ -166,7 +168,7 @@ def tile_list_rgg_ownP_kernel(
             return acc[:].rearrange("p (m t) -> p t m", t=PACK)
 
         def sigmoid(acc, name, jt):
-            eta = sb(name, [P, PACK, P], F32, "eta%d" % jt)
+            eta = sb(name, [P, PACK, P], F32)
             nc.scalar.activation(eta[:], dealt(acc), ACT.Sigmoid)
             return eta
 
@@ -174,17 +176,20 @@ def tile_list_rgg_ownP_kernel(
             return gate[:, h * TILES + jt : h * TILES + jt + 1]
 
         def message(dst, acc, eta, h, jt):
-            nc.vector.scalar_tensor_tensor(dst[:, jt], dealt(acc), gate_col(h, jt), eta[:], MULT, MULT)
+            nc.vector.scalar_tensor_tensor(dst[jt][:], dealt(acc), gate_col(h, jt), eta[:], MULT, MULT)
 
         def own(dst, acc, h, jt):
-            nc.scalar.activation(dst[:, jt], dealt(acc), ACT.Copy, scale=gate_col(h, jt))
+            nc.scalar.activation(dst[jt][:], dealt(acc), ACT.Copy, scale=gate_col(h, jt))
 
-        def turn(b, h, t, msg, ow, tag=None):
+        def turn(b, h, t, msg, ow):
             acc = bank(b, "turn%d%d" % (h, t))
             for jt in range(TILES):
                 cols = acc[:, jt * P : (jt + 1) * P]
-                nc.tensor.matmul(cols, ow[:, jt, t, :], ident[:], start=True, stop=False, is_transpose=True)
-                nc.tensor.matmul(cols, msg[:, jt, t, :], ident[:], start=False, stop=True, is_transpose=True)
+                nc.tensor.matmul(cols, ow[jt][:, t, :], ident[:], start=True, stop=False, is_transpose=True)
+                nc.tensor.matmul(cols, msg[jt][:, t, :], ident[:], start=False, stop=True, is_transpose=True)
+            return acc
+
+        def empty(acc, h, t, tag=None):
             vals = sb("vals%d%d" % (h, t), [P, HALF], F32, tag)
             nc.scalar.copy(vals[:], acc[:])
             return vals
@@ -201,89 +206,87 @@ def tile_list_rgg_ownP_kernel(
             for a in range(PASSES):
                 mx_pass(za[jt], 0, jt, 0, a, wb_q, False, a == PASSES - 1)
             eta.append(sigmoid(za[jt], "eta0%d" % jt, jt))
-        ms = [bank(jt, "ms0%d" % jt) for jt in range(TILES)]
-        msg0 = sb("msg0", [P, TILES, PACK, P], F32, "wo1_slot")
+        ms = [bank(TILES + jt, "ms0%d" % jt) for jt in range(TILES)]
+        msg0 = [sb("msg0%d" % jt, [P, PACK, P], F32) for jt in range(TILES)]
         for jt in range(TILES):
             for a in range(PASSES):
                 mx_pass(ms[jt], 0, jt, 0, a, wc_q, a == 0, a == PASSES - 1)
             message(msg0, ms[jt], eta[jt], 0, jt)
-        ow = [bank(TILES + jt, "ow0%d" % jt) for jt in range(TILES)]
-        own0 = sb("own0", [P, TILES, PACK, P], F32)
+        picked[1, 1] = gather_words(1, 1, "eta03")
+        ow = [bank(jt, "ow0%d" % jt) for jt in range(TILES)]
+        own0 = [sb("own0%d" % jt, [P, PACK, P], F32) for jt in range(TILES)]
         for jt in range(TILES):
             mx_pass(ow[jt], 0, jt, 1, 0, wo_q, True, False)
         for jt in range(TILES):
             mx_pass(ow[jt], 0, jt, 1, 1, wo_q, False, True)
             own(own0, ow[jt], 0, jt)
 
-        order = (2, 0, 1, 3)
         for b in range(3):
-            scatter(0, order[b], turn(b, 0, order[b], msg0, own0))
+            scatter(0, order[b], empty(turn(TILES + b, 0, order[b], msg0, own0), 0, order[b]))
+        held = turn(7, 0, order[3], msg0, own0)
 
         eta = []
         for jt in range(TILES):
-            acc = bank(3 + jt, "za1%d" % jt)
+            acc = bank(jt, "za1%d" % jt)
             for a in range(PASSES):
                 mx_pass(acc, 1, jt, 1, a, wa_q, a == 0, False)
             for a in range(PASSES):
                 mx_pass(acc, 1, jt, 0, a, wb_q, False, a == PASSES - 1)
             eta.append(sigmoid(acc, "eta1%d" % jt, jt))
-        own1 = sb("own1", [P, TILES, PACK, P], F32)
+        own1 = [sb("own1%d" % jt, [P, PACK, P], F32) for jt in range(TILES)]
         for jt in range(TILES):
-            acc = bank((7, 3, 4, 5)[jt], "ow1%d" % jt)
+            acc = bank((4, 5, 6, 0)[jt], "ow1%d" % jt)
             for a in range(PASSES):
                 mx_pass(acc, 1, jt, 1, a, wo_q, a == 0, a == PASSES - 1)
             own(own1, acc, 1, jt)
-        msg1 = sb("msg1", [P, TILES, PACK, P], F32)
+        msg1 = [sb("msg1%d" % jt, [P, PACK, P], F32) for jt in range(TILES)]
         for jt in range(TILES):
-            acc = bank((0, 1, 2, 6)[jt], "ms1%d" % jt)
+            acc = bank((1, 2, 3, 4)[jt], "ms1%d" % jt)
             for a in range(PASSES):
                 mx_pass(acc, 1, jt, 0, a, wc_q, a == 0, a == PASSES - 1)
             message(msg1, acc, eta[jt], 1, jt)
 
-        pairs = [sb("pairs%d" % c, [P, 2, CHUNK, 2], BF16) for c in range(CHUNKS)]
+        pairs = [sb("pairs%d" % s, [P, 2, T // 2, 2], BF16) for s in range(2)]
         out_rows = out_0.rearrange("(p t) c -> p t c", t=PACK)
 
-        def round_page(t, c, copy):
-            copy(pairs[c][:, t // 2, :, t % 2], pages[t][:, c * CHUNK : (c + 1) * CHUNK])
+        def round_page(t, s, copy):
+            copy(pairs[s][:, t // 2, :, t % 2], pages[t][:, s * T // 2 : (s + 1) * T // 2])
 
         def finish_page(t):
             nc.sync.dma_start(out_rows[:, t, :], pages[t][:])
-            for c in range(CHUNKS):
-                round_page(t, c, nc.scalar.copy)
+            for s in range(2):
+                round_page(t, s, nc.scalar.copy)
 
-        scatter(0, order[3], turn(0, 0, order[3], msg0, own0))
-        scatter(1, order[0], turn(7, 1, order[0], msg1, own1, "vals_last"))
-        vals_b = turn(3, 1, order[1], msg1, own1)
-        vals_c = turn(4, 1, order[2], msg1, own1)
-        finish_page(order[0])
-        scatter(1, order[1], vals_b)
-        vals_d = turn(5, 1, order[3], msg1, own1, "vals_last")
-        finish_page(order[1])
-        scatter(1, order[2], vals_c)
-        finish_page(order[2])
-        scatter(1, order[3], vals_d)
-
+        scatter(0, order[3], empty(held, 0, order[3], "eta12"))
+        vals = [empty(turn(b, 1, t, msg1, own1), 1, t) for b, t in zip((5, 6, 0, 7), order)]
+        for i in range(3):
+            scatter(1, order[i], vals[i])
+            finish_page(order[i])
         last = order[3]
+        scatter(1, last, vals[3])
+
         nc.sync.dma_start(out_rows[:, last, :], pages[last][:])
-        woven = [sb("woven%d" % c, [P, CHUNK, 2, 2], BF16) for c in range(CHUNKS)]
+        woven = [sb("woven%d" % c, [P, CHUNK, 2], U32) for c in range(CHUNKS)]
 
-        def weave(c, copy):
-            copy(woven[c][:], pairs[c][:].rearrange("p u c e -> p c u e"))
+        def weave(c, copy, word):
+            words = pairs[c // 2][:].rearrange("p u c e -> p u (c e)").bitcast(word)
+            cols = slice(c % 2 * CHUNK, (c % 2 + 1) * CHUNK)
+            copy(woven[c][:].bitcast(word), words[:, :, cols].rearrange("p u c -> p c u"))
 
-        for c in (2, 3):
-            round_page(last, c, nc.scalar.copy)
-            weave(c, nc.scalar.copy)
+        round_page(last, 1, nc.scalar.copy)
+        weave(2, nc.scalar.copy, U32)
+        round_page(last, 0, nc.vector.tensor_copy)
         for c in (0, 1):
-            round_page(last, c, nc.vector.tensor_copy)
-        for c in (0, 1):
-            weave(c, nc.vector.tensor_copy)
+            weave(c, nc.vector.tensor_copy, I32)
         out_s = sb("out_s", [P, T], U8)
         out_words = out_1[0].rearrange("p t i -> p (t i)").bitcast(I32)
         for c in range(CHUNKS):
+            if c == 2:
+                weave(3, nc.vector.tensor_copy, I32)
             cols = slice(c * CHUNK, (c + 1) * CHUNK)
             codes = sb("out_w%d" % c, [P, CHUNK], U32)
             nc.vector.quantize_mx(
-                out=codes[:].bitcast(FP8X4), scales=out_s[:, cols], in_=woven[c][:].rearrange("p c u e -> p (c u e)")
+                out=codes[:].bitcast(FP8X4), scales=out_s[:, cols], in_=woven[c][:].rearrange("p c u -> p (c u)").bitcast(BF16)
             )
             nc.sync.dma_start(out_words[:, cols], codes[:].bitcast(I32))
         for q in range(QUADS):

@@ -15,17 +15,19 @@ U8 = mybir.dt.uint8
 FP8X4 = mybir.dt.float8_e4m3fn_x4
 FP4X4 = mybir.dt.float4_e2m1fn_x4
 MULT = mybir.AluOpType.mult
+ADD = mybir.AluOpType.add
 ACT = mybir.ActivationFunctionType
 
 P = 128
 PACK = 4
 PASSES = K // (P * PACK)
-HALF = 512
-TILES = HALF // P
+TILES = J // P
+PAIR = 2 * P
+PAIRS = J // PAIR
 CHUNK = 512
 CHUNKS = T // CHUNK
 QUADS = 4
-SHIFT_ROWS = 100
+MIMIC = False
 
 
 def tile_list_rgg_ownP_kernel(
@@ -35,10 +37,25 @@ def tile_list_rgg_ownP_kernel(
     with ExitStack() as ctx:
         lists = ctx.enter_context(tc.tile_pool(name="lists", bufs=1))
         keep = ctx.enter_context(tc.tile_pool(name="keep", bufs=1))
+        staged = ctx.enter_context(tc.tile_pool(name="staged", bufs=1))
         psum = ctx.enter_context(tc.psum_pool(name="psum", bufs=1))
 
         def sb(name, shape, dtype, tag=None):
             return keep.tile(shape, dtype, name=name, tag=tag or name, align_bytes=64)
+
+        sizes = [("wa_raw0", 8192), ("wa_raw1", 8192), ("wo_raw0", 8192), ("wo_raw1", 8192), ("tab_w1", 8192), ("wb_w", 2048),
+                 ("wc_w", 4096), ("page0", 8192), ("page2", 8192), ("src_s", 1024), ("dst_s", 1024),
+                 ("picked00", 4096), ("picked10", 2048), ("wb_s", 1024), ("wc_s", 1024), ("src_s1", 1024), ("picked12", 2048)]
+        places = {name: sum(size for other, size in sizes[:i]) for i, (name, unused) in enumerate(sizes)}
+        span = sum(size for name, size in sizes)
+        for k in range(4):
+            places["eta%d" % k] = places["wo_raw0"] + 2048 * k
+        places["page1"] = places["wa_raw0"]
+        places["page3"] = places["wa_raw1"]
+        places["picked16"] = places["eta1"]
+
+        def late(name, shape, dtype, tag=None):
+            return staged.tile(shape, dtype, name=name, tag=tag or name, align_bytes=64, offset=places[tag or name])
 
         def bank(b, name):
             return psum.tile([P, N], F32, name=name, tag="bank%d" % b)
@@ -49,20 +66,35 @@ def tile_list_rgg_ownP_kernel(
         nc.sync.dma_start(dst_list[:], offs2)
         both_lists = (src_list, dst_list)
 
-        def half_list(lst, h):
-            return lst[:, h * HALF // 16 : (h + 1) * HALF // 16]
+        def entries(lst, first, last):
+            return lst[:, first * P // 16 : last * P // 16]
 
         tab_s = sb("tab_s", [P, T], U8)
         gate_rows = sb("gate_rows", [P, P], F32)
         ident = sb("ident", [P, P], F32)
-        nc.gpsimd.memset(tab_s[:].bitcast(I32), 0)
-        nc.gpsimd.memset(gate_rows[:], 0.0)
-        make_identity(nc, ident[:])
-        wb_s = sb("wb_s", [P, PASSES, N], U8)
-        wc_s = sb("wc_s", [P, PASSES, N], U8)
-        src_s1 = sb("src_s1", [P, J], U8)
-        for plane in (wb_s, wc_s, src_s1):
+        nc.vector.memset(tab_s[:].bitcast(I32), 0)
+        ident_draft = staged.tile([P, span // 4], F32, name="ident_draft", align_bytes=64, offset=0)
+        make_identity(nc, ident_draft[:, 0:P])
+        wb_s = late("wb_s", [P, PASSES, N], U8)
+        wc_s = late("wc_s", [P, PASSES, N], U8)
+        nc.vector.memset(gate_rows[:], 0.0)
+        nc.vector.tensor_copy(ident[:], ident_draft[:, 0:P])
+        src_s1 = late("src_s1", [P, J], U8)
+        for plane in (wc_s, wb_s, src_s1):
             nc.vector.memset(plane[:].bitcast(I32), 0)
+        order = (2, 0, 1, 3)
+        pages = {}
+
+        def clear_page(t, tag=None):
+            pages[t] = late("page%d" % t, [P, T], F32, tag)
+            if MIMIC and t in order[:2]:
+                nc.vector.memset(pages[t][:, 0 : T // 2].bitcast(I32), 0)
+                nc.gpsimd.memset(pages[t][:, T // 2 : T].bitcast(I32), 0)
+            else:
+                (nc.gpsimd if t in order[2:] else nc.vector).memset(pages[t][:].bitcast(I32), 0)
+
+        for t in order[:2]:
+            clear_page(t)
 
         for q in range(QUADS):
             nc.sync.dma_start(tab_s[32 * q : 32 * q + 8, :].bitcast(I32), tab_scales[:, 4 * q : 4 * q + 4, :].bitcast(I32))
@@ -75,88 +107,90 @@ def tile_list_rgg_ownP_kernel(
                 )
 
         def load_rows(w, a, name):
-            raw = sb(name, [P, PACK, N], F32)
+            raw = late(name, [P, PACK, N], F32)
             nc.sync.dma_start(raw[:], w[a * P * PACK : (a + 1) * P * PACK, :].rearrange("(p i) n -> p i n", i=PACK))
             return raw
 
         def load_table(a):
-            words = sb("tab_w%d" % a, [P, T], I32)
+            words = (sb, late)[a]("tab_w%d" % a, [P, T], I32)
             nc.sync.dma_start(words[:], tab_words[a].rearrange("p t i -> p (t i)").bitcast(I32))
             return words
 
-        wa_raw, wo_raw, tab_w = [], [], []
-        wa_raw.append(load_rows(wa, 0, "wa_raw0"))
+        wb_w = late("wb_w", [P, PASSES, 2 * N], U8)
+        wc_w = late("wc_w", [P, PASSES, N], U32)
+        tab_w, wa_raw, wo_raw = [], [], []
         tab_w.append(load_table(0))
-        nc.sync.dma_start(gate_rows[0 : J // P, :], wgo[0:1, :].rearrange("o (b c) -> (o b) c", c=P))
+        wa_raw.append(load_rows(wa, 0, "wa_raw0"))
         wa_raw.append(load_rows(wa, 1, "wa_raw1"))
+        nc.sync.dma_start(gate_rows[0:TILES, :], wgo[0:1, :].rearrange("o (b c) -> (o b) c", c=P))
         tab_w.append(load_table(1))
         load_scales(wb_s, wb_scales)
-        for a in range(PASSES):
-            wo_raw.append(load_rows(wo, a, "wo_raw%d" % a))
-        wb_w = sb("wb_w", [P, PASSES, 2 * N], U8)
         nc.sync.dma_start(wb_w[:].bitcast(I32), wb_words.rearrange("a p b -> p a b").bitcast(I32))
-        wc_w = sb("wc_w", [P, PASSES, N], U32)
-        nc.sync.dma_start(wc_w[:].bitcast(I32), wc_words.rearrange("a p n i -> p a (n i)").bitcast(I32))
+        wo_raw.append(load_rows(wo, 0, "wo_raw0"))
+        wo_raw.append(load_rows(wo, 1, "wo_raw1"))
         load_scales(wc_s, wc_scales)
+        nc.sync.dma_start(wc_w[:].bitcast(I32), wc_words.rearrange("a p n i -> p a (n i)").bitcast(I32))
 
-        src_s = sb("src_s", [P, J], U8)
-        dst_s = sb("dst_s", [P, J], U8)
-        nc.vector.tensor_copy(src_s[:], tab_s[:].indirect(src_list[:]))
-        nc.sync.dma_start(src_s1[0:SHIFT_ROWS, :].bitcast(I32), src_s[4 : 4 + SHIFT_ROWS, :].bitcast(I32))
-        nc.vector.tensor_copy(dst_s[:], tab_s[:].indirect(dst_list[:]))
+        src_s = late("src_s", [P, J], U8)
+        dst_s = late("dst_s", [P, J], U8)
 
         gate_ps = bank(7, "gate_ps")
         nc.tensor.transpose(gate_ps[:, 0:P], gate_rows[:], ident[:])
-        gate = sb("gate", [P, J // P], F32)
-        nc.scalar.copy(gate[:], gate_ps[:, 0 : J // P])
+        gate = sb("gate", [P, TILES], F32)
+        nc.scalar.copy(gate[:], gate_ps[:, 0:TILES])
 
-        order = (2, 0, 1, 3)
-        pages = {}
+        picked = {}
 
-        def clear_page(t, tag=None):
-            pages[t] = sb("page%d" % t, [P, T], F32, tag)
-            nc.vector.memset(pages[t][:].bitcast(I32), 0)
+        def gather_words(a, first, last, tag=None):
+            words = (sb if tag else late)("picked%d%d" % (a, first), [P, 2, (last - first) * P], U32, tag)
+            for s in (1, 0):
+                nc.vector.tensor_copy(words[:, s, :], tab_w[a][:].bitcast(U32).indirect(entries(both_lists[s], first, last)))
+            for k in range(first, last):
+                picked[a, k] = words[:, :, (k - first) * P : (k - first + 1) * P]
 
-        for t in order[:3]:
-            clear_page(t)
+        def pool_round(out, in_):
+            nc.gpsimd.tensor_scalar(out, in_, 1.0, 0.0, MULT, ADD)
 
-        def gather_words(h, a, tag=None):
-            picked = sb("picked%d%d" % (h, a), [P, 2, HALF], U32, tag)
-            for s in range(2):
-                nc.vector.tensor_copy(picked[:, s, :], tab_w[a][:].bitcast(U32).indirect(half_list(both_lists[s], h)))
-            return picked
-
-        def quantise_weight(raw, name):
-            grouped = sb(name + "_bf", [P, N, PACK], BF16, name + "_slot")
-            nc.scalar.copy(
-                grouped[:].rearrange("p (c e) i -> p c i e", e=4), raw[:].rearrange("p i (c e) -> p c i e", e=4)
-            )
+        def quantise_weight(raw, name, copies):
+            grouped = sb(name + "_bf", [P, N, PACK], BF16)
+            width = N // len(copies)
+            for j, copy in enumerate(copies):
+                cols = slice(j * width, (j + 1) * width)
+                copy(
+                    grouped[:, cols, :].rearrange("p (c e) i -> p c i e", e=4), raw[:, :, cols].rearrange("p i (c e) -> p c i e", e=4)
+                )
             codes = sb(name + "_codes", [P, N], U32)
             scales = sb(name + "_scales", [P, N], U8)
             nc.vector.quantize_mx(out=codes[:].bitcast(FP8X4), scales=scales[:], in_=grouped[:].rearrange("p n i -> p (n i)"))
             return codes[:].bitcast(FP8X4), scales[:]
 
-        picked = {}
-        picked[0, 0] = gather_words(0, 0)
-        wa_q = [quantise_weight(wa_raw[0], "wa0")]
-        picked[0, 1] = gather_words(0, 1)
-        wa_q.append(quantise_weight(wa_raw[1], "wa1"))
-        picked[1, 0] = gather_words(1, 0, "wa1_slot")
-        wo_q = [quantise_weight(wo_raw[0], "wo0")]
-        wo_q.append(quantise_weight(wo_raw[1], "wo1"))
-        clear_page(order[3], "wo1_slot")
+        wa_q, wo_q = [], []
+        nc.vector.tensor_copy(src_s[:], tab_s[:].indirect(src_list[:]))
+        nc.sync.dma_start(src_s1[0:100, :].bitcast(I32), src_s[4:104, :].bitcast(I32))
+        gather_words(0, 0, 4)
+        nc.vector.tensor_copy(dst_s[:], tab_s[:].indirect(dst_list[:]))
+        wa_q.append(quantise_weight(wa_raw[0], "wa0", [nc.scalar.copy]))
+        clear_page(order[2])
+        gather_words(1, 0, 2)
+        wa_q.append(quantise_weight(wa_raw[1], "wa1", [nc.scalar.copy]))
+        clear_page(order[3])
+        gather_words(1, 2, 4)
+        gather_words(0, 4, 8, "wa1_bf")
+        wo_q.append(quantise_weight(wo_raw[0], "wo0", [nc.scalar.copy]))
+        wo_q.append(quantise_weight(wo_raw[1], "wo1", [nc.vector.tensor_copy]))
+        gather_words(1, 4, 6, "wo1_bf")
         wb_q = [(wb_w[:, a, :].bitcast(FP4X4), wb_s[:, a, :]) for a in range(PASSES)]
         wc_q = [(wc_w[:, a, :].bitcast(FP8X4), wc_s[:, a, :]) for a in range(PASSES)]
 
-        def mx_pass(acc, h, jt, s, a, weight, start, stop):
-            cols = slice(h * HALF + jt * P, h * HALF + (jt + 1) * P)
-            if s == 0:
+        def mx_pass(acc, k, s, a, weight, start, stop):
+            cols = slice(k * P, (k + 1) * P)
+            if weight is wb_q:
                 plane = (src_s, src_s1)[a][:, cols]
             else:
-                plane = dst_s[4 * a : P, cols]
+                plane = (src_s, dst_s)[s][4 * a : P, cols]
             nc.tensor.matmul_mx(
                 out=acc[:],
-                lhsT=picked[h, a][:, s, jt * P : (jt + 1) * P].bitcast(FP8X4),
+                lhsT=picked[a, k][:, s, :].bitcast(FP8X4),
                 lhsT_scale=plane,
                 rhs=weight[a][0],
                 rhs_scale=weight[a][1],
@@ -167,122 +201,98 @@ def tile_list_rgg_ownP_kernel(
         def dealt(acc):
             return acc[:].rearrange("p (m t) -> p t m", t=PACK)
 
-        def sigmoid(acc, name, jt):
-            eta = sb(name, [P, PACK, P], F32)
-            nc.scalar.activation(eta[:], dealt(acc), ACT.Sigmoid)
-            return eta
+        msg, own = {}, {}
 
-        def gate_col(h, jt):
-            return gate[:, h * TILES + jt : h * TILES + jt + 1]
+        def message(k):
+            za = bank(k if k < 4 else 4 + k % 2, "za%d" % k)
+            for a in range(PASSES):
+                mx_pass(za, k, 1, a, wa_q, a == 0, False)
+            for a in range(PASSES):
+                mx_pass(za, k, 0, a, wb_q, False, a == PASSES - 1)
+            eta = (late if k < 4 else sb)("eta%d" % k, [P, PACK, P], F32)
+            nc.scalar.activation(eta[:], dealt(za), ACT.Sigmoid)
+            ms = bank(4 + k if k < 4 else 6 + k % 2, "ms%d" % k)
+            for a in range(PASSES):
+                mx_pass(ms, k, 0, a, wc_q, a == 0, a == PASSES - 1)
+            msg[k] = sb("msg%d" % k, [P, PACK, P], F32)
+            if k < 2:
+                nc.vector.scalar_tensor_tensor(msg[k][:], dealt(ms), gate[:, k : k + 1], eta[:], MULT, MULT)
+            else:
+                scaled = sb("scaled%d" % k, [P, PACK, P], F32)
+                nc.scalar.activation(scaled[:], dealt(ms), ACT.Copy, scale=gate[:, k : k + 1])
+                nc.gpsimd.tensor_tensor(msg[k][:], scaled[:], eta[:], MULT)
 
-        def message(dst, acc, eta, h, jt):
-            nc.vector.scalar_tensor_tensor(dst[jt][:], dealt(acc), gate_col(h, jt), eta[:], MULT, MULT)
+        def projection(k):
+            ow = bank(k if k < 4 else 2 + k % 2, "ow%d" % k)
+            for a in range(PASSES):
+                mx_pass(ow, k, 1, a, wo_q, a == 0, a == PASSES - 1)
+            own[k] = sb("own%d" % k, [P, PACK, P], F32)
+            nc.scalar.activation(own[k][:], dealt(ow), ACT.Copy, scale=gate[:, k : k + 1])
 
-        def own(dst, acc, h, jt):
-            nc.scalar.activation(dst[jt][:], dealt(acc), ACT.Copy, scale=gate_col(h, jt))
-
-        def turn(b, h, t, msg, ow):
-            acc = bank(b, "turn%d%d" % (h, t))
-            for jt in range(TILES):
-                cols = acc[:, jt * P : (jt + 1) * P]
-                nc.tensor.matmul(cols, ow[jt][:, t, :], ident[:], start=True, stop=False, is_transpose=True)
-                nc.tensor.matmul(cols, msg[jt][:, t, :], ident[:], start=False, stop=True, is_transpose=True)
-            return acc
-
-        def empty(acc, h, t, tag=None):
-            vals = sb("vals%d%d" % (h, t), [P, HALF], F32, tag)
-            nc.scalar.copy(vals[:], acc[:])
+        def turn(b, pieces, tag=None):
+            name = "%d%d" % pieces[0][0:2]
+            acc = bank(b, "turn" + name)
+            col = 0
+            for t, first, last in pieces:
+                for k in range(first, last):
+                    cols = acc[:, col : col + P]
+                    nc.tensor.matmul(cols, own[k][:, t, :], ident[:], start=True, stop=False, is_transpose=True)
+                    nc.tensor.matmul(cols, msg[k][:, t, :], ident[:], start=False, stop=True, is_transpose=True)
+                    col = col + P
+            vals = sb("vals" + name, [P, col], F32, tag)
+            nc.scalar.copy(vals[:], acc[:, 0:col])
             return vals
 
-        def scatter(h, t, vals):
-            nc.vector.tensor_copy(pages[t][:].indirect(half_list(dst_list, h)), vals[:])
+        def scatter(vals, pieces):
+            col = 0
+            for t, first, last in pieces:
+                width = (last - first) * P
+                nc.vector.tensor_copy(pages[t][:].indirect(entries(dst_list, first, last)), vals[:, col : col + width])
+                col = col + width
 
-        za = [bank(jt, "za0%d" % jt) for jt in range(TILES)]
-        for a in range(PASSES):
-            for jt in range(TILES):
-                mx_pass(za[jt], 0, jt, 1, a, wa_q, a == 0, False)
-        eta = []
-        for jt in range(TILES):
-            for a in range(PASSES):
-                mx_pass(za[jt], 0, jt, 0, a, wb_q, False, a == PASSES - 1)
-            eta.append(sigmoid(za[jt], "eta0%d" % jt, jt))
-        ms = [bank(TILES + jt, "ms0%d" % jt) for jt in range(TILES)]
-        msg0 = [sb("msg0%d" % jt, [P, PACK, P], F32) for jt in range(TILES)]
-        for jt in range(TILES):
-            for a in range(PASSES):
-                mx_pass(ms[jt], 0, jt, 0, a, wc_q, a == 0, a == PASSES - 1)
-            message(msg0, ms[jt], eta[jt], 0, jt)
-        picked[1, 1] = gather_words(1, 1, "eta03")
-        ow = [bank(jt, "ow0%d" % jt) for jt in range(TILES)]
-        own0 = [sb("own0%d" % jt, [P, PACK, P], F32) for jt in range(TILES)]
-        for jt in range(TILES):
-            mx_pass(ow[jt], 0, jt, 1, 0, wo_q, True, False)
-        for jt in range(TILES):
-            mx_pass(ow[jt], 0, jt, 1, 1, wo_q, False, True)
-            own(own0, ow[jt], 0, jt)
+        for g in range(PAIRS):
+            for k in (2 * g, 2 * g + 1):
+                message(k)
+            for k in (2 * g, 2 * g + 1):
+                projection(k)
+            if g == 0:
+                gather_words(1, 6, 8)
+            for u in range(2):
+                pieces = [(t, 2 * g, 2 * g + 2) for t in order[2 * u : 2 * u + 2] if g < 2 or t != order[3]]
+                scatter(turn(u, pieces), pieces)
+        pieces = [(order[3], 4, 8)]
+        scatter(turn(4, pieces, "vals26"), pieces)
 
-        for b in range(3):
-            scatter(0, order[b], empty(turn(TILES + b, 0, order[b], msg0, own0), 0, order[b]))
-        held = turn(7, 0, order[3], msg0, own0)
-
-        eta = []
-        for jt in range(TILES):
-            acc = bank(jt, "za1%d" % jt)
-            for a in range(PASSES):
-                mx_pass(acc, 1, jt, 1, a, wa_q, a == 0, False)
-            for a in range(PASSES):
-                mx_pass(acc, 1, jt, 0, a, wb_q, False, a == PASSES - 1)
-            eta.append(sigmoid(acc, "eta1%d" % jt, jt))
-        own1 = [sb("own1%d" % jt, [P, PACK, P], F32) for jt in range(TILES)]
-        for jt in range(TILES):
-            acc = bank((4, 5, 6, 0)[jt], "ow1%d" % jt)
-            for a in range(PASSES):
-                mx_pass(acc, 1, jt, 1, a, wo_q, a == 0, a == PASSES - 1)
-            own(own1, acc, 1, jt)
-        msg1 = [sb("msg1%d" % jt, [P, PACK, P], F32) for jt in range(TILES)]
-        for jt in range(TILES):
-            acc = bank((1, 2, 3, 4)[jt], "ms1%d" % jt)
-            for a in range(PASSES):
-                mx_pass(acc, 1, jt, 0, a, wc_q, a == 0, a == PASSES - 1)
-            message(msg1, acc, eta[jt], 1, jt)
-
-        pairs = [sb("pairs%d" % s, [P, 2, T // 2, 2], BF16) for s in range(2)]
+        pairs = [sb("pairs%d" % c, [P, 2, CHUNK, 2], BF16) for c in range(CHUNKS)]
         out_rows = out_0.rearrange("(p t) c -> p t c", t=PACK)
 
-        def round_page(t, s, copy):
-            copy(pairs[s][:, t // 2, :, t % 2], pages[t][:, s * T // 2 : (s + 1) * T // 2])
+        def round_page(t, c, copy):
+            copy(pairs[c][:, t // 2, :, t % 2], pages[t][:, c * CHUNK : (c + 1) * CHUNK])
 
-        def finish_page(t):
+        for i, t in enumerate(order):
             nc.sync.dma_start(out_rows[:, t, :], pages[t][:])
-            for s in range(2):
-                round_page(t, s, nc.scalar.copy)
-
-        scatter(0, order[3], empty(held, 0, order[3], "eta12"))
-        vals = [empty(turn(b, 1, t, msg1, own1), 1, t) for b, t in zip((5, 6, 0, 7), order)]
-        for i in range(3):
-            scatter(1, order[i], vals[i])
-            finish_page(order[i])
+            if i < PACK - 1:
+                for c in range(CHUNKS):
+                    round_page(t, c, pool_round if i > 0 and c < 2 else nc.scalar.copy)
         last = order[3]
-        scatter(1, last, vals[3])
 
-        nc.sync.dma_start(out_rows[:, last, :], pages[last][:])
-        woven = [sb("woven%d" % c, [P, CHUNK, 2], U32) for c in range(CHUNKS)]
+        woven = [sb("woven%d" % c, [P, CHUNK, 2], U32, ("wa0_bf", "wa1_bf", "wo0_bf", "wo1_bf")[c]) for c in range(CHUNKS)]
 
         def weave(c, copy, word):
-            words = pairs[c // 2][:].rearrange("p u c e -> p u (c e)").bitcast(word)
-            cols = slice(c % 2 * CHUNK, (c % 2 + 1) * CHUNK)
-            copy(woven[c][:].bitcast(word), words[:, :, cols].rearrange("p u c -> p c u"))
+            words = pairs[c][:].rearrange("p u c e -> p u (c e)").bitcast(word)
+            copy(woven[c][:].bitcast(word), words.rearrange("p u c -> p c u"))
 
-        round_page(last, 1, nc.scalar.copy)
-        weave(2, nc.scalar.copy, U32)
         round_page(last, 0, nc.vector.tensor_copy)
+        for c in range(1, CHUNKS):
+            round_page(last, c, nc.scalar.copy)
+        weave(3, nc.scalar.copy, U32)
         for c in (0, 1):
             weave(c, nc.vector.tensor_copy, I32)
         out_s = sb("out_s", [P, T], U8)
         out_words = out_1[0].rearrange("p t i -> p (t i)").bitcast(I32)
         for c in range(CHUNKS):
             if c == 2:
-                weave(3, nc.vector.tensor_copy, I32)
+                weave(2, nc.vector.tensor_copy, I32)
             cols = slice(c * CHUNK, (c + 1) * CHUNK)
             codes = sb("out_w%d" % c, [P, CHUNK], U32)
             nc.vector.quantize_mx(

@@ -43,15 +43,17 @@ def tile_list_rgg_ownP_kernel(
         def sb(name, shape, dtype, tag=None):
             return keep.tile(shape, dtype, name=name, tag=tag or name, align_bytes=64)
 
-        sizes = [("wa_raw0", 8192), ("wa_raw1", 8192), ("wo_raw0", 8192), ("wo_raw1", 8192), ("tab_w1", 8192), ("wb_w", 2048),
-                 ("wc_w", 4096), ("page0", 8192), ("page2", 8192), ("src_s", 1024), ("dst_s", 1024),
-                 ("picked00", 4096), ("picked10", 2048), ("wb_s", 1024), ("wc_s", 1024), ("src_s1", 1024), ("picked12", 2048)]
+        sizes = [("wa_raw0", 8192), ("tab_w1", 8192), ("wa_raw1", 8192), ("wb_w", 2048), ("page0", 8192), ("page2", 8192), ("src_s", 1024), ("dst_s", 1024),
+                 ("picked00", 2048), ("picked02", 2048), ("picked10", 2048), ("wb_s", 1024), ("src_s1", 1024), ("picked12", 2048)]
         places = {name: sum(size for other, size in sizes[:i]) for i, (name, unused) in enumerate(sizes)}
         span = sum(size for name, size in sizes)
+        behind = [("tab_s", 2048), ("wo_raw0", 8192), ("wo_raw1", 8192), ("wc_w", 4096), ("wc_s", 1024)]
+        for i, (name, unused) in enumerate(behind):
+            places[name] = span + sum(size for other, size in behind[:i])
         for k in range(4):
-            places["eta%d" % k] = places["wo_raw0"] + 2048 * k
-        places["page1"] = places["wa_raw0"]
-        places["page3"] = places["wa_raw1"]
+            places["eta%d" % k] = places["wo_raw1"] + 2048 * k
+        places["page1"] = places["tab_w1"] - 4096
+        places["page3"] = places["tab_w1"] + 4096
         places["picked16"] = places["eta1"]
 
         def late(name, shape, dtype, tag=None):
@@ -69,32 +71,28 @@ def tile_list_rgg_ownP_kernel(
         def entries(lst, first, last):
             return lst[:, first * P // 16 : last * P // 16]
 
-        tab_s = sb("tab_s", [P, T], U8)
+        tab_s = late("tab_s", [P, sum(size for name, size in behind)], U8)[:, 0:T]
         gate_rows = sb("gate_rows", [P, P], F32)
         ident = sb("ident", [P, P], F32)
-        nc.vector.memset(tab_s[:].bitcast(I32), 0)
+        nc.vector.memset(tab_s.bitcast(I32), 0)
         ident_draft = staged.tile([P, span // 4], F32, name="ident_draft", align_bytes=64, offset=0)
         make_identity(nc, ident_draft[:, 0:P])
         wb_s = late("wb_s", [P, PASSES, N], U8)
-        wc_s = late("wc_s", [P, PASSES, N], U8)
         nc.vector.memset(gate_rows[:], 0.0)
         nc.vector.tensor_copy(ident[:], ident_draft[:, 0:P])
         src_s1 = late("src_s1", [P, J], U8)
-        for plane in (wc_s, wb_s, src_s1):
+        for plane in (src_s1, wb_s):
             nc.vector.memset(plane[:].bitcast(I32), 0)
         order = (2, 0, 1, 3)
         pages = {}
 
-        def clear_page(t, tag=None):
-            pages[t] = late("page%d" % t, [P, T], F32, tag)
-            if MIMIC and t in order[:2]:
-                nc.vector.memset(pages[t][:, 0 : T // 2].bitcast(I32), 0)
-                nc.gpsimd.memset(pages[t][:, T // 2 : T].bitcast(I32), 0)
-            else:
-                (nc.gpsimd if t in order[2:] else nc.vector).memset(pages[t][:].bitcast(I32), 0)
+
+        def clear_page(t, engine):
+            pages[t] = late("page%d" % t, [P, T], F32)
+            engine.memset(pages[t][:].bitcast(I32), 0)
 
         for t in order[:2]:
-            clear_page(t)
+            clear_page(t, nc.vector)
 
         for q in range(QUADS):
             nc.sync.dma_start(tab_s[32 * q : 32 * q + 8, :].bitcast(I32), tab_scales[:, 4 * q : 4 * q + 4, :].bitcast(I32))
@@ -117,7 +115,6 @@ def tile_list_rgg_ownP_kernel(
             return words
 
         wb_w = late("wb_w", [P, PASSES, 2 * N], U8)
-        wc_w = late("wc_w", [P, PASSES, N], U32)
         tab_w, wa_raw, wo_raw = [], [], []
         tab_w.append(load_table(0))
         wa_raw.append(load_rows(wa, 0, "wa_raw0"))
@@ -126,10 +123,6 @@ def tile_list_rgg_ownP_kernel(
         tab_w.append(load_table(1))
         load_scales(wb_s, wb_scales)
         nc.sync.dma_start(wb_w[:].bitcast(I32), wb_words.rearrange("a p b -> p a b").bitcast(I32))
-        wo_raw.append(load_rows(wo, 0, "wo_raw0"))
-        wo_raw.append(load_rows(wo, 1, "wo_raw1"))
-        load_scales(wc_s, wc_scales)
-        nc.sync.dma_start(wc_w[:].bitcast(I32), wc_words.rearrange("a p n i -> p a (n i)").bitcast(I32))
 
         src_s = late("src_s", [P, J], U8)
         dst_s = late("dst_s", [P, J], U8)
@@ -151,7 +144,7 @@ def tile_list_rgg_ownP_kernel(
         def pool_round(out, in_):
             nc.gpsimd.tensor_scalar(out, in_, 1.0, 0.0, MULT, ADD)
 
-        def quantise_weight(raw, name, copies):
+        def round_weight(raw, name, copies):
             grouped = sb(name + "_bf", [P, N, PACK], BF16)
             width = N // len(copies)
             for j, copy in enumerate(copies):
@@ -159,26 +152,35 @@ def tile_list_rgg_ownP_kernel(
                 copy(
                     grouped[:, cols, :].rearrange("p (c e) i -> p c i e", e=4), raw[:, :, cols].rearrange("p i (c e) -> p c i e", e=4)
                 )
+            return grouped
+
+        def quantise_weight(grouped, name):
             codes = sb(name + "_codes", [P, N], U32)
             scales = sb(name + "_scales", [P, N], U8)
             nc.vector.quantize_mx(out=codes[:].bitcast(FP8X4), scales=scales[:], in_=grouped[:].rearrange("p n i -> p (n i)"))
             return codes[:].bitcast(FP8X4), scales[:]
 
         wa_q, wo_q = [], []
-        nc.vector.tensor_copy(src_s[:], tab_s[:].indirect(src_list[:]))
+        gather_words(0, 0, 2)
+        nc.vector.tensor_copy(src_s[:], tab_s.indirect(src_list[:]))
         nc.sync.dma_start(src_s1[0:100, :].bitcast(I32), src_s[4:104, :].bitcast(I32))
-        gather_words(0, 0, 4)
-        nc.vector.tensor_copy(dst_s[:], tab_s[:].indirect(dst_list[:]))
-        wa_q.append(quantise_weight(wa_raw[0], "wa0", [nc.scalar.copy]))
-        clear_page(order[2])
+        nc.vector.tensor_copy(dst_s[:], tab_s.indirect(dst_list[:]))
+        wo_raw.append(load_rows(wo, 0, "wo_raw0"))
+        wo_raw.append(load_rows(wo, 1, "wo_raw1"))
+        wc_w = late("wc_w", [P, PASSES, N], U32)
+        nc.sync.dma_start(wc_w[:].bitcast(I32), wc_words.rearrange("a p n i -> p a (n i)").bitcast(I32))
+        wc_s = late("wc_s", [P, PASSES, N], U8)
+        nc.vector.memset(wc_s[:].bitcast(I32), 0)
+        load_scales(wc_s, wc_scales)
+        gather_words(0, 2, 4)
+        wa_q.append(quantise_weight(round_weight(wa_raw[0], "wa0", [nc.scalar.copy]), "wa0"))
         gather_words(1, 0, 2)
-        wa_q.append(quantise_weight(wa_raw[1], "wa1", [nc.scalar.copy]))
-        clear_page(order[3])
+        wa_q.append(quantise_weight(round_weight(wa_raw[1], "wa1", [nc.scalar.copy]), "wa1"))
         gather_words(1, 2, 4)
         gather_words(0, 4, 8, "wa1_bf")
-        wo_q.append(quantise_weight(wo_raw[0], "wo0", [nc.scalar.copy]))
-        wo_q.append(quantise_weight(wo_raw[1], "wo1", [nc.vector.tensor_copy]))
-        gather_words(1, 4, 6, "wo1_bf")
+        wo_q.append(quantise_weight(round_weight(wo_raw[0], "wo0", [nc.scalar.copy]), "wo0"))
+        gather_words(1, 4, 6, "wo0_bf")
+        wo_q.append(quantise_weight(round_weight(wo_raw[1], "wo1", [nc.scalar.copy]), "wo1"))
         wb_q = [(wb_w[:, a, :].bitcast(FP4X4), wb_s[:, a, :]) for a in range(PASSES)]
         wc_q = [(wc_w[:, a, :].bitcast(FP8X4), wc_s[:, a, :]) for a in range(PASSES)]
 
@@ -204,26 +206,25 @@ def tile_list_rgg_ownP_kernel(
         msg, own = {}, {}
 
         def message(k):
-            za = bank(k if k < 4 else 4 + k % 2, "za%d" % k)
+            za = bank(k if k < 4 else 6 + k % 2, "za%d" % k)
             for a in range(PASSES):
                 mx_pass(za, k, 1, a, wa_q, a == 0, False)
-            for a in range(PASSES):
                 mx_pass(za, k, 0, a, wb_q, False, a == PASSES - 1)
-            eta = (late if k < 4 else sb)("eta%d" % k, [P, PACK, P], F32)
-            nc.scalar.activation(eta[:], dealt(za), ACT.Sigmoid)
-            ms = bank(4 + k if k < 4 else 6 + k % 2, "ms%d" % k)
+            eta = (late if k < 4 else sb)("eta%d" % k, [P, PACK, P], F32)[:]
+            nc.scalar.activation(eta, dealt(za), ACT.Sigmoid)
+            ms = bank(4 + k % 2, "ms%d" % k)
             for a in range(PASSES):
                 mx_pass(ms, k, 0, a, wc_q, a == 0, a == PASSES - 1)
             msg[k] = sb("msg%d" % k, [P, PACK, P], F32)
-            if k < 2:
-                nc.vector.scalar_tensor_tensor(msg[k][:], dealt(ms), gate[:, k : k + 1], eta[:], MULT, MULT)
+            if k < 4:
+                nc.vector.scalar_tensor_tensor(msg[k][:], dealt(ms), gate[:, k : k + 1], eta, MULT, MULT)
             else:
                 scaled = sb("scaled%d" % k, [P, PACK, P], F32)
                 nc.scalar.activation(scaled[:], dealt(ms), ACT.Copy, scale=gate[:, k : k + 1])
-                nc.gpsimd.tensor_tensor(msg[k][:], scaled[:], eta[:], MULT)
+                nc.gpsimd.tensor_tensor(msg[k][:], scaled[:], eta, MULT)
 
         def projection(k):
-            ow = bank(k if k < 4 else 2 + k % 2, "ow%d" % k)
+            ow = bank(6 + k if k < 2 else 2 + k % 2, "ow%d" % k)
             for a in range(PASSES):
                 mx_pass(ow, k, 1, a, wo_q, a == 0, a == PASSES - 1)
             own[k] = sb("own%d" % k, [P, PACK, P], F32)
@@ -250,41 +251,40 @@ def tile_list_rgg_ownP_kernel(
                 nc.vector.tensor_copy(pages[t][:].indirect(entries(dst_list, first, last)), vals[:, col : col + width])
                 col = col + width
 
+        for k in range(2):
+            message(k)
+        gather_words(1, 6, 8)
+        for t in order[2:]:
+            clear_page(t, nc.gpsimd)
         for g in range(PAIRS):
             for k in (2 * g, 2 * g + 1):
-                message(k)
-            for k in (2 * g, 2 * g + 1):
                 projection(k)
-            if g == 0:
-                gather_words(1, 6, 8)
+            for k in range(2 * g + 2, min(2 * g + 4, TILES)):
+                message(k)
             for u in range(2):
                 pieces = [(t, 2 * g, 2 * g + 2) for t in order[2 * u : 2 * u + 2] if g < 2 or t != order[3]]
                 scatter(turn(u, pieces), pieces)
         pieces = [(order[3], 4, 8)]
         scatter(turn(4, pieces, "vals26"), pieces)
 
-        pairs = [sb("pairs%d" % c, [P, 2, CHUNK, 2], BF16) for c in range(CHUNKS)]
+        pairs = [sb("pairs%d" % h, [P, 2, T // 2, 2], BF16) for h in range(2)]
         out_rows = out_0.rearrange("(p t) c -> p t c", t=PACK)
 
-        def round_page(t, c, copy):
-            copy(pairs[c][:, t // 2, :, t % 2], pages[t][:, c * CHUNK : (c + 1) * CHUNK])
+        def round_page(t, h, copy):
+            copy(pairs[h][:, t // 2, :, t % 2], pages[t][:, h * T // 2 : (h + 1) * T // 2])
 
         for i, t in enumerate(order):
             nc.sync.dma_start(out_rows[:, t, :], pages[t][:])
-            if i < PACK - 1:
-                for c in range(CHUNKS):
-                    round_page(t, c, pool_round if i > 0 and c < 2 else nc.scalar.copy)
-        last = order[3]
+            round_page(t, 0, (nc.scalar.copy, pool_round, pool_round, nc.vector.tensor_copy)[i])
+            round_page(t, 1, nc.scalar.copy)
 
         woven = [sb("woven%d" % c, [P, CHUNK, 2], U32, ("wa0_bf", "wa1_bf", "wo0_bf", "wo1_bf")[c]) for c in range(CHUNKS)]
 
         def weave(c, copy, word):
-            words = pairs[c][:].rearrange("p u c e -> p u (c e)").bitcast(word)
-            copy(woven[c][:].bitcast(word), words.rearrange("p u c -> p c u"))
+            words = pairs[c // 2][:].rearrange("p u c e -> p u (c e)").bitcast(word)
+            cols = slice(c % 2 * CHUNK, (c % 2 + 1) * CHUNK)
+            copy(woven[c][:].bitcast(word), words[:, :, cols].rearrange("p u c -> p c u"))
 
-        round_page(last, 0, nc.vector.tensor_copy)
-        for c in range(1, CHUNKS):
-            round_page(last, c, nc.scalar.copy)
         weave(3, nc.scalar.copy, U32)
         for c in (0, 1):
             weave(c, nc.vector.tensor_copy, I32)

@@ -22,12 +22,17 @@ P = 128
 PACK = 4
 PASSES = K // (P * PACK)
 TILES = J // P
-PAIR = 2 * P
-PAIRS = J // PAIR
+PAIRS = TILES // 2
+QUADS = 4
+GROUP = 16
 CHUNK = 512
 CHUNKS = T // CHUNK
-QUADS = 4
-MIMIC = False
+SRC, DST = 0, 1
+SHIFT_ROWS = 3 * 32 + 4
+KIB = 1024
+
+PAGE_ORDER = (2, 0, 1, 3)
+LAST_PAGE = PAGE_ORDER[-1]
 
 
 def tile_list_rgg_ownP_kernel(
@@ -43,56 +48,56 @@ def tile_list_rgg_ownP_kernel(
         def sb(name, shape, dtype, tag=None):
             return keep.tile(shape, dtype, name=name, tag=tag or name, align_bytes=64)
 
-        sizes = [("wa_raw0", 8192), ("tab_w1", 8192), ("wa_raw1", 8192), ("wb_w", 2048), ("page0", 8192), ("page2", 8192), ("src_s", 1024), ("dst_s", 1024),
-                 ("picked00", 2048), ("picked02", 2048), ("picked10", 2048), ("wb_s", 1024), ("src_s1", 1024), ("picked12", 2048)]
-        places = {name: sum(size for other, size in sizes[:i]) for i, (name, unused) in enumerate(sizes)}
-        span = sum(size for name, size in sizes)
-        behind = [("tab_s", 2048), ("wo_raw0", 8192), ("wo_raw1", 8192), ("wc_w", 4096), ("wc_s", 1024)]
-        for i, (name, unused) in enumerate(behind):
-            places[name] = span + sum(size for other, size in behind[:i])
+        after_identity = [
+            ("wa_raw0", 8), ("tab_w1", 8), ("wa_raw1", 8), ("wb_w", 2), ("wo_raw0", 8), ("wo_raw1", 4),
+            ("page0", 8), ("page1", 8), ("page2", 8), ("src_s", 1), ("dst_s", 1),
+            ("picked00", 2), ("picked02", 2), ("picked10", 2), ("wb_s", 1), ("wc_s", 1), ("src_s1", 1), ("picked12", 2),
+        ]
+        after_scales = [("tab_s", 2), ("wo_raw2", 4), ("wc_w", 4)]
+        placed = after_identity + after_scales
+        places = {name: KIB * sum(size for other, size in placed[:i]) for i, (name, unused) in enumerate(placed)}
         for k in range(4):
-            places["eta%d" % k] = places["wo_raw1"] + 2048 * k
-        places["page1"] = places["tab_w1"] - 4096
-        places["page3"] = places["tab_w1"] + 4096
+            places["eta%d" % k] = places["wo_raw1"] + 2 * KIB * (k - 2)
         places["picked16"] = places["eta1"]
+        places["page%d" % LAST_PAGE] = places["tab_w1"]
 
-        def late(name, shape, dtype, tag=None):
-            return staged.tile(shape, dtype, name=name, tag=tag or name, align_bytes=64, offset=places[tag or name])
+        def at_place(name, shape, dtype):
+            return staged.tile(shape, dtype, name=name, tag=name, align_bytes=64, offset=places[name])
 
         def bank(b, name):
             return psum.tile([P, N], F32, name=name, tag="bank%d" % b)
 
-        src_list = lists.tile([P, J // 16], U16, name="src_list")
-        dst_list = lists.tile([P, J // 16], U16, name="dst_list")
+        src_list = lists.tile([P, J // GROUP], U16, name="src_list")
+        dst_list = lists.tile([P, J // GROUP], U16, name="dst_list")
         nc.sync.dma_start(src_list[:], offs)
         nc.sync.dma_start(dst_list[:], offs2)
         both_lists = (src_list, dst_list)
 
         def entries(lst, first, last):
-            return lst[:, first * P // 16 : last * P // 16]
+            return lst[:, first * P // GROUP : last * P // GROUP]
 
-        tab_s = late("tab_s", [P, sum(size for name, size in behind)], U8)[:, 0:T]
+        tab_s = at_place("tab_s", [P, KIB * sum(size for name, size in after_scales)], U8)[:, 0:T]
         gate_rows = sb("gate_rows", [P, P], F32)
         ident = sb("ident", [P, P], F32)
         nc.vector.memset(tab_s.bitcast(I32), 0)
-        ident_draft = staged.tile([P, span // 4], F32, name="ident_draft", align_bytes=64, offset=0)
+        ident_draft = staged.tile([P, places["tab_s"] // 4], F32, name="ident_draft", align_bytes=64, offset=0)
         make_identity(nc, ident_draft[:, 0:P])
-        wb_s = late("wb_s", [P, PASSES, N], U8)
+        wb_s = at_place("wb_s", [P, PASSES, N], U8)
         nc.vector.memset(gate_rows[:], 0.0)
         nc.vector.tensor_copy(ident[:], ident_draft[:, 0:P])
-        src_s1 = late("src_s1", [P, J], U8)
-        for plane in (src_s1, wb_s):
+        src_s1 = at_place("src_s1", [P, J], U8)
+        wc_s = at_place("wc_s", [P, PASSES, N], U8)
+        for plane in (src_s1, wb_s, wc_s):
             nc.vector.memset(plane[:].bitcast(I32), 0)
-        order = (2, 0, 1, 3)
+
         pages = {}
 
+        def clear_page(t):
+            pages[t] = at_place("page%d" % t, [P, T], F32)
+            nc.vector.memset(pages[t][:].bitcast(I32), 0)
 
-        def clear_page(t, engine):
-            pages[t] = late("page%d" % t, [P, T], F32)
-            engine.memset(pages[t][:].bitcast(I32), 0)
-
-        for t in order[:2]:
-            clear_page(t, nc.vector)
+        for t in PAGE_ORDER[:-1]:
+            clear_page(t)
 
         for q in range(QUADS):
             nc.sync.dma_start(tab_s[32 * q : 32 * q + 8, :].bitcast(I32), tab_scales[:, 4 * q : 4 * q + 4, :].bitcast(I32))
@@ -104,28 +109,29 @@ def tile_list_rgg_ownP_kernel(
                     scales[:, 4 * q : 4 * q + 4, :].rearrange("a r n -> r a n").bitcast(I32),
                 )
 
-        def load_rows(w, a, name):
-            raw = late(name, [P, PACK, N], F32)
-            nc.sync.dma_start(raw[:], w[a * P * PACK : (a + 1) * P * PACK, :].rearrange("(p i) n -> p i n", i=PACK))
+        def load_rows(w, a, name, cols=slice(0, N)):
+            raw = at_place(name, [P, PACK, cols.stop - cols.start], F32)
+            nc.sync.dma_start(raw[:], w[a * P * PACK : (a + 1) * P * PACK, cols].rearrange("(p i) n -> p i n", i=PACK))
             return raw
 
         def load_table(a):
-            words = (sb, late)[a]("tab_w%d" % a, [P, T], I32)
+            words = (sb, at_place)[a]("tab_w%d" % a, [P, T], I32)
             nc.sync.dma_start(words[:], tab_words[a].rearrange("p t i -> p (t i)").bitcast(I32))
             return words
 
-        wb_w = late("wb_w", [P, PASSES, 2 * N], U8)
-        tab_w, wa_raw, wo_raw = [], [], []
-        tab_w.append(load_table(0))
-        wa_raw.append(load_rows(wa, 0, "wa_raw0"))
-        wa_raw.append(load_rows(wa, 1, "wa_raw1"))
+        wb_w = at_place("wb_w", [P, PASSES, 2 * N], U8)
+        tab_w = [load_table(0)]
+        wa_raw = [load_rows(wa, a, "wa_raw%d" % a) for a in range(PASSES)]
         nc.sync.dma_start(gate_rows[0:TILES, :], wgo[0:1, :].rearrange("o (b c) -> (o b) c", c=P))
         tab_w.append(load_table(1))
         load_scales(wb_s, wb_scales)
         nc.sync.dma_start(wb_w[:].bitcast(I32), wb_words.rearrange("a p b -> p a b").bitcast(I32))
+        wo_first = load_rows(wo, 0, "wo_raw0")
+        load_scales(wc_s, wc_scales)
+        wo_second = [load_rows(wo, 1, "wo_raw1", slice(0, N // 2))]
 
-        src_s = late("src_s", [P, J], U8)
-        dst_s = late("dst_s", [P, J], U8)
+        src_s = at_place("src_s", [P, J], U8)
+        dst_s = at_place("dst_s", [P, J], U8)
 
         gate_ps = bank(7, "gate_ps")
         nc.tensor.transpose(gate_ps[:, 0:P], gate_rows[:], ident[:])
@@ -135,52 +141,42 @@ def tile_list_rgg_ownP_kernel(
         picked = {}
 
         def gather_words(a, first, last, tag=None):
-            words = (sb if tag else late)("picked%d%d" % (a, first), [P, 2, (last - first) * P], U32, tag)
-            for s in (1, 0):
+            name, shape = "picked%d%d" % (a, first), [P, 2, (last - first) * P]
+            words = sb(name, shape, U32, tag) if tag else at_place(name, shape, U32)
+            for s in (DST, SRC):
                 nc.vector.tensor_copy(words[:, s, :], tab_w[a][:].bitcast(U32).indirect(entries(both_lists[s], first, last)))
             for k in range(first, last):
                 picked[a, k] = words[:, :, (k - first) * P : (k - first + 1) * P]
 
-        def pool_round(out, in_):
-            nc.gpsimd.tensor_scalar(out, in_, 1.0, 0.0, MULT, ADD)
-
-        def round_weight(raw, name, copies):
+        def quantise_weight(raws, name, copies):
             grouped = sb(name + "_bf", [P, N, PACK], BF16)
-            width = N // len(copies)
-            for j, copy in enumerate(copies):
-                cols = slice(j * width, (j + 1) * width)
-                copy(
-                    grouped[:, cols, :].rearrange("p (c e) i -> p c i e", e=4), raw[:, :, cols].rearrange("p i (c e) -> p c i e", e=4)
-                )
-            return grouped
-
-        def quantise_weight(grouped, name):
             codes = sb(name + "_codes", [P, N], U32)
             scales = sb(name + "_scales", [P, N], U8)
-            nc.vector.quantize_mx(out=codes[:].bitcast(FP8X4), scales=scales[:], in_=grouped[:].rearrange("p n i -> p (n i)"))
+            width = N // len(raws)
+            for j, raw in enumerate(raws):
+                cols = slice(j * width, (j + 1) * width)
+                copies[j](grouped[:, cols, :].rearrange("p (c e) i -> p c i e", e=4), raw[:].rearrange("p i (c e) -> p c i e", e=4))
+                nc.vector.quantize_mx(
+                    out=codes[:, cols].bitcast(FP8X4), scales=scales[:, cols], in_=grouped[:, cols, :].rearrange("p n i -> p (n i)")
+                )
             return codes[:].bitcast(FP8X4), scales[:]
 
-        wa_q, wo_q = [], []
         gather_words(0, 0, 2)
         nc.vector.tensor_copy(src_s[:], tab_s.indirect(src_list[:]))
-        nc.sync.dma_start(src_s1[0:100, :].bitcast(I32), src_s[4:104, :].bitcast(I32))
+        nc.sync.dma_start(src_s1[0:SHIFT_ROWS, :].bitcast(I32), src_s[4 : 4 + SHIFT_ROWS, :].bitcast(I32))
         nc.vector.tensor_copy(dst_s[:], tab_s.indirect(dst_list[:]))
-        wo_raw.append(load_rows(wo, 0, "wo_raw0"))
-        wo_raw.append(load_rows(wo, 1, "wo_raw1"))
-        wc_w = late("wc_w", [P, PASSES, N], U32)
+        wo_second.append(load_rows(wo, 1, "wo_raw2", slice(N // 2, N)))
+        wc_w = at_place("wc_w", [P, PASSES, N], U32)
         nc.sync.dma_start(wc_w[:].bitcast(I32), wc_words.rearrange("a p n i -> p a (n i)").bitcast(I32))
-        wc_s = late("wc_s", [P, PASSES, N], U8)
-        nc.vector.memset(wc_s[:].bitcast(I32), 0)
-        load_scales(wc_s, wc_scales)
         gather_words(0, 2, 4)
-        wa_q.append(quantise_weight(round_weight(wa_raw[0], "wa0", [nc.scalar.copy]), "wa0"))
+        wa_q = [quantise_weight([wa_raw[0]], "wa0", [nc.scalar.copy])]
         gather_words(1, 0, 2)
-        wa_q.append(quantise_weight(round_weight(wa_raw[1], "wa1", [nc.scalar.copy]), "wa1"))
+        wa_q.append(quantise_weight([wa_raw[1]], "wa1", [nc.scalar.copy]))
         gather_words(1, 2, 4)
         gather_words(0, 4, 8, "wa1_bf")
-        wo_q.append(quantise_weight(round_weight(wo_raw[0], "wo0", [nc.scalar.copy]), "wo0"))
+        wo_q = [quantise_weight([wo_first], "wo0", [nc.scalar.copy])]
         gather_words(1, 4, 6, "wo0_bf")
-        wo_q.append(quantise_weight(round_weight(wo_raw[1], "wo1", [nc.scalar.copy]), "wo1"))
+        wo_q.append(quantise_weight(wo_second, "wo1", [nc.scalar.copy, nc.vector.tensor_copy]))
         wb_q = [(wb_w[:, a, :].bitcast(FP4X4), wb_s[:, a, :]) for a in range(PASSES)]
         wc_q = [(wc_w[:, a, :].bitcast(FP8X4), wc_s[:, a, :]) for a in range(PASSES)]
 
@@ -208,29 +204,29 @@ def tile_list_rgg_ownP_kernel(
         def message(k):
             za = bank(k if k < 4 else 6 + k % 2, "za%d" % k)
             for a in range(PASSES):
-                mx_pass(za, k, 1, a, wa_q, a == 0, False)
-                mx_pass(za, k, 0, a, wb_q, False, a == PASSES - 1)
-            eta = (late if k < 4 else sb)("eta%d" % k, [P, PACK, P], F32)[:]
-            nc.scalar.activation(eta, dealt(za), ACT.Sigmoid)
+                mx_pass(za, k, DST, a, wa_q, a == 0, False)
+                mx_pass(za, k, SRC, a, wb_q, False, a == PASSES - 1)
+            eta = (at_place if k < 4 else sb)("eta%d" % k, [P, PACK, P], F32)
+            nc.scalar.activation(eta[:], dealt(za), ACT.Sigmoid)
             ms = bank(4 + k % 2, "ms%d" % k)
             for a in range(PASSES):
-                mx_pass(ms, k, 0, a, wc_q, a == 0, a == PASSES - 1)
+                mx_pass(ms, k, SRC, a, wc_q, a == 0, a == PASSES - 1)
             msg[k] = sb("msg%d" % k, [P, PACK, P], F32)
-            if k < 4:
-                nc.vector.scalar_tensor_tensor(msg[k][:], dealt(ms), gate[:, k : k + 1], eta, MULT, MULT)
+            if k < 2:
+                nc.vector.scalar_tensor_tensor(msg[k][:], dealt(ms), gate[:, k : k + 1], eta[:], MULT, MULT)
             else:
                 scaled = sb("scaled%d" % k, [P, PACK, P], F32)
                 nc.scalar.activation(scaled[:], dealt(ms), ACT.Copy, scale=gate[:, k : k + 1])
-                nc.gpsimd.tensor_tensor(msg[k][:], scaled[:], eta, MULT)
+                nc.gpsimd.tensor_tensor(msg[k][:], scaled[:], eta[:], MULT)
 
         def projection(k):
             ow = bank(6 + k if k < 2 else 2 + k % 2, "ow%d" % k)
             for a in range(PASSES):
-                mx_pass(ow, k, 1, a, wo_q, a == 0, a == PASSES - 1)
+                mx_pass(ow, k, DST, a, wo_q, a == 0, a == PASSES - 1)
             own[k] = sb("own%d" % k, [P, PACK, P], F32)
             nc.scalar.activation(own[k][:], dealt(ow), ACT.Copy, scale=gate[:, k : k + 1])
 
-        def turn(b, pieces, tag=None):
+        def place_results(b, pieces, tag=None):
             name = "%d%d" % pieces[0][0:2]
             acc = bank(b, "turn" + name)
             col = 0
@@ -242,9 +238,6 @@ def tile_list_rgg_ownP_kernel(
                     col = col + P
             vals = sb("vals" + name, [P, col], F32, tag)
             nc.scalar.copy(vals[:], acc[:, 0:col])
-            return vals
-
-        def scatter(vals, pieces):
             col = 0
             for t, first, last in pieces:
                 width = (last - first) * P
@@ -254,28 +247,30 @@ def tile_list_rgg_ownP_kernel(
         for k in range(2):
             message(k)
         gather_words(1, 6, 8)
-        for t in order[2:]:
-            clear_page(t, nc.gpsimd)
+        clear_page(LAST_PAGE)
         for g in range(PAIRS):
             for k in (2 * g, 2 * g + 1):
                 projection(k)
             for k in range(2 * g + 2, min(2 * g + 4, TILES)):
                 message(k)
             for u in range(2):
-                pieces = [(t, 2 * g, 2 * g + 2) for t in order[2 * u : 2 * u + 2] if g < 2 or t != order[3]]
-                scatter(turn(u, pieces), pieces)
-        pieces = [(order[3], 4, 8)]
-        scatter(turn(4, pieces, "vals26"), pieces)
+                two_pages = PAGE_ORDER[2 * u : 2 * u + 2]
+                place_results(u, [(t, 2 * g, 2 * g + 2) for t in two_pages if g < PAIRS // 2 or t != LAST_PAGE])
+        place_results(4, [(LAST_PAGE, TILES // 2, TILES)], "vals%d%d" % (PAGE_ORDER[0], TILES - 2))
 
         pairs = [sb("pairs%d" % h, [P, 2, T // 2, 2], BF16) for h in range(2)]
         out_rows = out_0.rearrange("(p t) c -> p t c", t=PACK)
 
+        def gpsimd_round(out, in_):
+            nc.gpsimd.tensor_scalar(out, in_, 1.0, -0.0, MULT, ADD)
+
         def round_page(t, h, copy):
             copy(pairs[h][:, t // 2, :, t % 2], pages[t][:, h * T // 2 : (h + 1) * T // 2])
 
-        for i, t in enumerate(order):
+        first_half_by = (gpsimd_round, gpsimd_round, nc.scalar.copy, nc.vector.tensor_copy)
+        for t in PAGE_ORDER:
             nc.sync.dma_start(out_rows[:, t, :], pages[t][:])
-            round_page(t, 0, (nc.scalar.copy, pool_round, pool_round, nc.vector.tensor_copy)[i])
+            round_page(t, 0, first_half_by[t])
             round_page(t, 1, nc.scalar.copy)
 
         woven = [sb("woven%d" % c, [P, CHUNK, 2], U32, ("wa0_bf", "wa1_bf", "wo0_bf", "wo1_bf")[c]) for c in range(CHUNKS)]
@@ -285,14 +280,14 @@ def tile_list_rgg_ownP_kernel(
             cols = slice(c % 2 * CHUNK, (c % 2 + 1) * CHUNK)
             copy(woven[c][:].bitcast(word), words[:, :, cols].rearrange("p u c -> p c u"))
 
-        weave(3, nc.scalar.copy, U32)
-        for c in (0, 1):
+        weave(CHUNKS - 1, nc.scalar.copy, U32)
+        for c in range(CHUNKS // 2):
             weave(c, nc.vector.tensor_copy, I32)
         out_s = sb("out_s", [P, T], U8)
         out_words = out_1[0].rearrange("p t i -> p (t i)").bitcast(I32)
         for c in range(CHUNKS):
-            if c == 2:
-                weave(2, nc.vector.tensor_copy, I32)
+            if c == CHUNKS // 2:
+                weave(c, nc.vector.tensor_copy, I32)
             cols = slice(c * CHUNK, (c + 1) * CHUNK)
             codes = sb("out_w%d" % c, [P, CHUNK], U32)
             nc.vector.quantize_mx(

@@ -50,16 +50,17 @@ def tile_list_rgg_ownP_kernel(
 
         after_identity = [
             ("wa_raw0", 8), ("tab_w1", 8), ("wa_raw1", 8), ("wb_w", 2), ("wo_raw0", 8), ("wo_raw1", 4),
-            ("page0", 8), ("page1", 8), ("page2", 8), ("src_s", 1), ("dst_s", 1),
+            ("page0", 8), ("page2", 8), ("src_s", 1), ("dst_s", 1),
             ("picked00", 2), ("picked02", 2), ("picked10", 2), ("wb_s", 1), ("wc_s", 1), ("src_s1", 1), ("picked12", 2),
         ]
         after_scales = [("tab_s", 2), ("wo_raw2", 4), ("wc_w", 4)]
-        placed = after_identity + after_scales
+        after_gate = [("page%d" % t, 8) for t in PAGE_ORDER[2:]]
+        placed = after_identity + after_scales + after_gate
         places = {name: KIB * sum(size for other, size in placed[:i]) for i, (name, unused) in enumerate(placed)}
         for k in range(4):
             places["eta%d" % k] = places["wo_raw1"] + 2 * KIB * (k - 2)
-        places["picked16"] = places["eta1"]
-        places["page%d" % LAST_PAGE] = places["tab_w1"]
+        places["picked14"] = places["eta0"]
+        places["gate_rows"] = places[after_gate[0][0]]
 
         def at_place(name, shape, dtype):
             return staged.tile(shape, dtype, name=name, tag=name, align_bytes=64, offset=places[name])
@@ -77,13 +78,13 @@ def tile_list_rgg_ownP_kernel(
             return lst[:, first * P // GROUP : last * P // GROUP]
 
         tab_s = at_place("tab_s", [P, KIB * sum(size for name, size in after_scales)], U8)[:, 0:T]
-        gate_rows = sb("gate_rows", [P, P], F32)
+        gate_rows = at_place("gate_rows", [P, 2 * T], F32)[:, 0:P]
         ident = sb("ident", [P, P], F32)
         nc.vector.memset(tab_s.bitcast(I32), 0)
         ident_draft = staged.tile([P, places["tab_s"] // 4], F32, name="ident_draft", align_bytes=64, offset=0)
         make_identity(nc, ident_draft[:, 0:P])
         wb_s = at_place("wb_s", [P, PASSES, N], U8)
-        nc.vector.memset(gate_rows[:], 0.0)
+        nc.vector.memset(gate_rows, 0.0)
         nc.vector.tensor_copy(ident[:], ident_draft[:, 0:P])
         src_s1 = at_place("src_s1", [P, J], U8)
         wc_s = at_place("wc_s", [P, PASSES, N], U8)
@@ -92,12 +93,12 @@ def tile_list_rgg_ownP_kernel(
 
         pages = {}
 
-        def clear_page(t):
+        def clear_page(t, engine):
             pages[t] = at_place("page%d" % t, [P, T], F32)
-            nc.vector.memset(pages[t][:].bitcast(I32), 0)
+            engine.memset(pages[t][:].bitcast(I32), 0)
 
-        for t in PAGE_ORDER[:-1]:
-            clear_page(t)
+        for t in PAGE_ORDER[:2]:
+            clear_page(t, nc.vector)
 
         for q in range(QUADS):
             nc.sync.dma_start(tab_s[32 * q : 32 * q + 8, :].bitcast(I32), tab_scales[:, 4 * q : 4 * q + 4, :].bitcast(I32))
@@ -121,22 +122,25 @@ def tile_list_rgg_ownP_kernel(
 
         wb_w = at_place("wb_w", [P, PASSES, 2 * N], U8)
         tab_w = [load_table(0)]
-        wa_raw = [load_rows(wa, a, "wa_raw%d" % a) for a in range(PASSES)]
+        wa_raw = []
+        for a, (plane, scales) in enumerate(((wb_s, wb_scales), (wc_s, wc_scales))):
+            wa_raw.append(load_rows(wa, a, "wa_raw%d" % a))
+            load_scales(plane, scales)
         nc.sync.dma_start(gate_rows[0:TILES, :], wgo[0:1, :].rearrange("o (b c) -> (o b) c", c=P))
         tab_w.append(load_table(1))
-        load_scales(wb_s, wb_scales)
         nc.sync.dma_start(wb_w[:].bitcast(I32), wb_words.rearrange("a p b -> p a b").bitcast(I32))
         wo_first = load_rows(wo, 0, "wo_raw0")
-        load_scales(wc_s, wc_scales)
         wo_second = [load_rows(wo, 1, "wo_raw1", slice(0, N // 2))]
 
         src_s = at_place("src_s", [P, J], U8)
         dst_s = at_place("dst_s", [P, J], U8)
 
         gate_ps = bank(7, "gate_ps")
-        nc.tensor.transpose(gate_ps[:, 0:P], gate_rows[:], ident[:])
+        nc.tensor.transpose(gate_ps[:, 0:P], gate_rows, ident[:])
         gate = sb("gate", [P, TILES], F32)
         nc.scalar.copy(gate[:], gate_ps[:, 0:TILES])
+        for t in PAGE_ORDER[2:]:
+            clear_page(t, nc.gpsimd)
 
         picked = {}
 
@@ -175,7 +179,6 @@ def tile_list_rgg_ownP_kernel(
         gather_words(1, 2, 4)
         gather_words(0, 4, 8, "wa1_bf")
         wo_q = [quantise_weight([wo_first], "wo0", [nc.scalar.copy])]
-        gather_words(1, 4, 6, "wo0_bf")
         wo_q.append(quantise_weight(wo_second, "wo1", [nc.scalar.copy, nc.vector.tensor_copy]))
         wb_q = [(wb_w[:, a, :].bitcast(FP4X4), wb_s[:, a, :]) for a in range(PASSES)]
         wc_q = [(wc_w[:, a, :].bitcast(FP8X4), wc_s[:, a, :]) for a in range(PASSES)]
@@ -202,7 +205,7 @@ def tile_list_rgg_ownP_kernel(
         msg, own = {}, {}
 
         def message(k):
-            za = bank(k if k < 4 else 6 + k % 2, "za%d" % k)
+            za = bank(k if k < 4 else k % 2, "za%d" % k)
             for a in range(PASSES):
                 mx_pass(za, k, DST, a, wa_q, a == 0, False)
                 mx_pass(za, k, SRC, a, wb_q, False, a == PASSES - 1)
@@ -244,18 +247,23 @@ def tile_list_rgg_ownP_kernel(
                 nc.vector.tensor_copy(pages[t][:].indirect(entries(dst_list, first, last)), vals[:, col : col + width])
                 col = col + width
 
+        def place_pair(g, u):
+            two_pages = PAGE_ORDER[2 * u : 2 * u + 2]
+            place_results(u if g == 0 else 6 + u, [(t, 2 * g, 2 * g + 2) for t in two_pages if g < PAIRS // 2 or t != LAST_PAGE])
+
         for k in range(2):
             message(k)
-        gather_words(1, 6, 8)
-        clear_page(LAST_PAGE)
+        gather_words(1, 4, 8)
         for g in range(PAIRS):
             for k in (2 * g, 2 * g + 1):
                 projection(k)
+            if g == 0:
+                place_pair(g, 0)
             for k in range(2 * g + 2, min(2 * g + 4, TILES)):
                 message(k)
-            for u in range(2):
-                two_pages = PAGE_ORDER[2 * u : 2 * u + 2]
-                place_results(u, [(t, 2 * g, 2 * g + 2) for t in two_pages if g < PAIRS // 2 or t != LAST_PAGE])
+            if g > 0:
+                place_pair(g, 0)
+            place_pair(g, 1)
         place_results(4, [(LAST_PAGE, TILES // 2, TILES)], "vals%d%d" % (PAGE_ORDER[0], TILES - 2))
 
         pairs = [sb("pairs%d" % h, [P, 2, T // 2, 2], BF16) for h in range(2)]

@@ -48,19 +48,26 @@ def tile_list_rgg_ownP_kernel(
         def sb(name, shape, dtype, tag=None):
             return keep.tile(shape, dtype, name=name, tag=tag or name, align_bytes=64)
 
-        after_identity = [
-            ("wa_raw0", 8), ("tab_w1", 8), ("wa_raw1", 8), ("wb_w", 2), ("wo_raw0", 8), ("wo_raw1", 4),
-            ("page0", 8), ("page2", 8), ("src_s", 1), ("dst_s", 1),
-            ("picked00", 2), ("picked02", 2), ("picked10", 2), ("wb_s", 1), ("wc_s", 1), ("src_s1", 1), ("picked12", 2),
-        ]
-        after_scales = [("tab_s", 2), ("wo_raw2", 4), ("wc_w", 4)]
-        after_gate = [("page%d" % t, 8) for t in PAGE_ORDER[2:]]
-        placed = after_identity + after_scales + after_gate
+        first = [("tab_w0", 8), ("wb_s", 1), ("gate_rows", 1)]
+        second = [("wa_raw0", 8), ("wa_raw1", 8), ("wc_s", 2), ("src_s1", 2), ("src_s", 1), ("dst_s", 1)]
+        second = second + [("page%d" % t, 8) for t in PAGE_ORDER[:3]]
+        after_scales = [("tab_s", 2), ("tab_w1", 8), ("wo_raw0", 8), ("wo_raw1", 4), ("wo_raw2", 4), ("wc_w", 4)]
+        rounded = [("wa0_bf0", 4), ("wa1_bf0", 4), ("wo0_bf0", 4), ("wo1_bf0", 4), ("wo1_bf1", 2)]
+        placed = first + second + after_scales + rounded
         places = {name: KIB * sum(size for other, size in placed[:i]) for i, (name, unused) in enumerate(placed)}
+        places["draft0"] = places[first[0][0]]
+        places["draft1"] = places[second[0][0]]
         for k in range(4):
-            places["eta%d" % k] = places["wo_raw1"] + 2 * KIB * (k - 2)
-        places["picked14"] = places["eta0"]
-        places["gate_rows"] = places[after_gate[0][0]]
+            places["eta%d" % k] = places["wo_raw0"] + 2 * KIB * (k % 2)
+        places["gate"] = places["wa_raw1"]
+        places["picked04"] = places["wa0_bf0"]
+        places["picked12"] = places["wa1_bf0"]
+        places["picked16"] = places["wo1_bf1"]
+        places["page%d" % LAST_PAGE] = places["wo0_bf0"]
+        for h in range(2):
+            places["pairs%d" % h] = places["tab_w%d" % h]
+        for c in range(CHUNKS):
+            places["woven%d" % c] = places["wa_raw0"] + 4 * KIB * c
 
         def at_place(name, shape, dtype):
             return staged.tile(shape, dtype, name=name, tag=name, align_bytes=64, offset=places[name])
@@ -77,29 +84,37 @@ def tile_list_rgg_ownP_kernel(
         def entries(lst, first, last):
             return lst[:, first * P // GROUP : last * P // GROUP]
 
-        tab_s = at_place("tab_s", [P, KIB * sum(size for name, size in after_scales)], U8)[:, 0:T]
-        gate_rows = at_place("gate_rows", [P, 2 * T], F32)[:, 0:P]
-        ident = sb("ident", [P, P], F32)
+        def region(name, parts, dtype, size):
+            return at_place(name, [P, KIB * sum(kib for other, kib in parts) // size], dtype)
+
+        tab_s = region("tab_s", after_scales, U8, 1)[:, 0:T]
         nc.vector.memset(tab_s.bitcast(I32), 0)
-        ident_draft = staged.tile([P, places["tab_s"] // 4], F32, name="ident_draft", align_bytes=64, offset=0)
-        make_identity(nc, ident_draft[:, 0:P])
+        drafts = [region("draft0", first, F32, 4)[:, 0:P], region("draft1", second, F32, 4)[:, 0:P]]
+        ident = sb("ident", [P, P], F32)
+        make_identity(nc, drafts[0])
+        nc.vector.tensor_copy(drafts[1], drafts[0])
         wb_s = at_place("wb_s", [P, PASSES, N], U8)
-        nc.vector.memset(gate_rows, 0.0)
-        nc.vector.tensor_copy(ident[:], ident_draft[:, 0:P])
-        src_s1 = at_place("src_s1", [P, J], U8)
-        wc_s = at_place("wc_s", [P, PASSES, N], U8)
-        for plane in (src_s1, wb_s, wc_s):
+        nc.vector.memset(wb_s[:].bitcast(I32), 0)
+        gate_rows = at_place("gate_rows", [P, P], F32)
+        nc.vector.memset(gate_rows[:], 0.0)
+        nc.vector.tensor_copy(ident[:], drafts[1])
+        planes = [at_place(name, [P, J + 4], U8) for name in ("wc_s", "src_s1")]
+        for plane in planes:
             nc.vector.memset(plane[:].bitcast(I32), 0)
+        wc_s = planes[0][:, 0:J].rearrange("p (a n) -> p a n", a=PASSES)
+        src_s1 = planes[1][:, 0:J]
 
         pages = {}
 
-        def clear_page(t, engine):
+        def clear_page(t):
             pages[t] = at_place("page%d" % t, [P, T], F32)
-            engine.memset(pages[t][:].bitcast(I32), 0)
+            nc.gpsimd.memset(pages[t][:].bitcast(I32), 0)
 
-        for t in PAGE_ORDER[:2]:
-            clear_page(t, nc.vector)
+        for t in PAGE_ORDER[:3]:
+            clear_page(t)
 
+        wb_w = sb("wb_w", [P, PASSES, 2 * N], U8)
+        nc.sync.dma_start(wb_w[:].bitcast(I32), wb_words.rearrange("a p b -> p a b").bitcast(I32))
         for q in range(QUADS):
             nc.sync.dma_start(tab_s[32 * q : 32 * q + 8, :].bitcast(I32), tab_scales[:, 4 * q : 4 * q + 4, :].bitcast(I32))
 
@@ -116,70 +131,65 @@ def tile_list_rgg_ownP_kernel(
             return raw
 
         def load_table(a):
-            words = (sb, at_place)[a]("tab_w%d" % a, [P, T], I32)
+            words = at_place("tab_w%d" % a, [P, T], I32)
             nc.sync.dma_start(words[:], tab_words[a].rearrange("p t i -> p (t i)").bitcast(I32))
             return words
 
-        wb_w = at_place("wb_w", [P, PASSES, 2 * N], U8)
         tab_w = [load_table(0)]
-        wa_raw = []
-        for a, (plane, scales) in enumerate(((wb_s, wb_scales), (wc_s, wc_scales))):
-            wa_raw.append(load_rows(wa, a, "wa_raw%d" % a))
-            load_scales(plane, scales)
+        load_scales(wb_s, wb_scales)
         nc.sync.dma_start(gate_rows[0:TILES, :], wgo[0:1, :].rearrange("o (b c) -> (o b) c", c=P))
-        tab_w.append(load_table(1))
-        nc.sync.dma_start(wb_w[:].bitcast(I32), wb_words.rearrange("a p b -> p a b").bitcast(I32))
-        wo_first = load_rows(wo, 0, "wo_raw0")
-        wo_second = [load_rows(wo, 1, "wo_raw1", slice(0, N // 2))]
+        wa_raw = [load_rows(wa, a, "wa_raw%d" % a) for a in range(PASSES)]
+        load_scales(wc_s, wc_scales)
 
         src_s = at_place("src_s", [P, J], U8)
         dst_s = at_place("dst_s", [P, J], U8)
 
         gate_ps = bank(7, "gate_ps")
-        nc.tensor.transpose(gate_ps[:, 0:P], gate_rows, ident[:])
-        gate = sb("gate", [P, TILES], F32)
+        nc.tensor.transpose(gate_ps[:, 0:P], gate_rows[:], ident[:])
+        gate = at_place("gate", [P, TILES], F32)
         nc.scalar.copy(gate[:], gate_ps[:, 0:TILES])
-        for t in PAGE_ORDER[2:]:
-            clear_page(t, nc.gpsimd)
 
         picked = {}
 
-        def gather_words(a, first, last, tag=None):
+        def gather_words(a, first, last):
             name, shape = "picked%d%d" % (a, first), [P, 2, (last - first) * P]
-            words = sb(name, shape, U32, tag) if tag else at_place(name, shape, U32)
+            words = (at_place if name in places else sb)(name, shape, U32)
             for s in (DST, SRC):
                 nc.vector.tensor_copy(words[:, s, :], tab_w[a][:].bitcast(U32).indirect(entries(both_lists[s], first, last)))
             for k in range(first, last):
                 picked[a, k] = words[:, :, (k - first) * P : (k - first + 1) * P]
 
         def quantise_weight(raws, name, copies):
-            grouped = sb(name + "_bf", [P, N, PACK], BF16)
             codes = sb(name + "_codes", [P, N], U32)
             scales = sb(name + "_scales", [P, N], U8)
             width = N // len(raws)
             for j, raw in enumerate(raws):
                 cols = slice(j * width, (j + 1) * width)
-                copies[j](grouped[:, cols, :].rearrange("p (c e) i -> p c i e", e=4), raw[:].rearrange("p i (c e) -> p c i e", e=4))
+                grouped = at_place("%s_bf%d" % (name, j), [P, width, PACK], BF16)
+                copies[j](grouped[:].rearrange("p (c e) i -> p c i e", e=4), raw[:].rearrange("p i (c e) -> p c i e", e=4))
                 nc.vector.quantize_mx(
-                    out=codes[:, cols].bitcast(FP8X4), scales=scales[:, cols], in_=grouped[:, cols, :].rearrange("p n i -> p (n i)")
+                    out=codes[:, cols].bitcast(FP8X4), scales=scales[:, cols], in_=grouped[:].rearrange("p n i -> p (n i)")
                 )
             return codes[:].bitcast(FP8X4), scales[:]
 
-        gather_words(0, 0, 2)
         nc.vector.tensor_copy(src_s[:], tab_s.indirect(src_list[:]))
         nc.sync.dma_start(src_s1[0:SHIFT_ROWS, :].bitcast(I32), src_s[4 : 4 + SHIFT_ROWS, :].bitcast(I32))
         nc.vector.tensor_copy(dst_s[:], tab_s.indirect(dst_list[:]))
-        wo_second.append(load_rows(wo, 1, "wo_raw2", slice(N // 2, N)))
+        tab_w.append(load_table(1))
+        wo_first = load_rows(wo, 0, "wo_raw0")
+        wo_second = [load_rows(wo, 1, "wo_raw%d" % (1 + h), slice(h * N // 2, (h + 1) * N // 2)) for h in range(2)]
         wc_w = at_place("wc_w", [P, PASSES, N], U32)
         nc.sync.dma_start(wc_w[:].bitcast(I32), wc_words.rearrange("a p n i -> p a (n i)").bitcast(I32))
+        gather_words(0, 0, 2)
         gather_words(0, 2, 4)
         wa_q = [quantise_weight([wa_raw[0]], "wa0", [nc.scalar.copy])]
-        gather_words(1, 0, 2)
+        gather_words(0, 4, 8)
         wa_q.append(quantise_weight([wa_raw[1]], "wa1", [nc.scalar.copy]))
-        gather_words(1, 2, 4)
-        gather_words(0, 4, 8, "wa1_bf")
+        gather_words(1, 0, 2)
+        gather_words(1, 2, 6)
         wo_q = [quantise_weight([wo_first], "wo0", [nc.scalar.copy])]
         wo_q.append(quantise_weight(wo_second, "wo1", [nc.scalar.copy, nc.vector.tensor_copy]))
+        clear_page(LAST_PAGE)
         wb_q = [(wb_w[:, a, :].bitcast(FP4X4), wb_s[:, a, :]) for a in range(PASSES)]
         wc_q = [(wc_w[:, a, :].bitcast(FP8X4), wc_s[:, a, :]) for a in range(PASSES)]
 
@@ -253,7 +263,7 @@ def tile_list_rgg_ownP_kernel(
 
         for k in range(2):
             message(k)
-        gather_words(1, 4, 8)
+        gather_words(1, 6, 8)
         for g in range(PAIRS):
             for k in (2 * g, 2 * g + 1):
                 projection(k)
@@ -266,7 +276,7 @@ def tile_list_rgg_ownP_kernel(
             place_pair(g, 1)
         place_results(4, [(LAST_PAGE, TILES // 2, TILES)], "vals%d%d" % (PAGE_ORDER[0], TILES - 2))
 
-        pairs = [sb("pairs%d" % h, [P, 2, T // 2, 2], BF16) for h in range(2)]
+        pairs = [at_place("pairs%d" % h, [P, 2, T // 2, 2], BF16) for h in range(2)]
         out_rows = out_0.rearrange("(p t) c -> p t c", t=PACK)
 
         def gpsimd_round(out, in_):
@@ -281,7 +291,7 @@ def tile_list_rgg_ownP_kernel(
             round_page(t, 0, first_half_by[t])
             round_page(t, 1, nc.scalar.copy)
 
-        woven = [sb("woven%d" % c, [P, CHUNK, 2], U32, ("wa0_bf", "wa1_bf", "wo0_bf", "wo1_bf")[c]) for c in range(CHUNKS)]
+        woven = [at_place("woven%d" % c, [P, CHUNK, 2], U32) for c in range(CHUNKS)]
 
         def weave(c, copy, word):
             words = pairs[c // 2][:].rearrange("p u c e -> p u (c e)").bitcast(word)

@@ -49,20 +49,22 @@ def tile_list_rgg_ownP_kernel(
             return keep.tile(shape, dtype, name=name, tag=tag or name, align_bytes=64)
 
         first = [("tab_w0", 8), ("wb_s", 1), ("gate_rows", 1)]
-        second = [("wa_raw0", 8), ("wa_raw1", 8), ("wc_s", 2), ("src_s1", 2), ("src_s", 1), ("dst_s", 1)]
+        second = [("wa_raw0", 8), ("wa_raw1", 8), ("wc_s", 1), ("src_s", 1), ("dst_s", 1)]
         second = second + [("page%d" % t, 8) for t in PAGE_ORDER[:3]]
-        after_scales = [("tab_s", 2), ("tab_w1", 8), ("wo_raw0", 8), ("wo_raw1", 4), ("wo_raw2", 4), ("wc_w", 4)]
-        rounded = [("wa0_bf0", 4), ("wa1_bf0", 4), ("wo0_bf0", 4), ("wo1_bf0", 4), ("wo1_bf1", 2)]
+        after_scales = [("tab_s", 2), ("tab_w1", 8), ("wo_raw00", 8), ("wo_raw10", 4), ("wo_raw11", 4), ("wc_w", 4)]
+        rounded = [("wa0_bf0", 4), ("wa1_bf0", 4), ("wo0_bf0", 4), ("wo1_bf0", 2), ("wo1_bf1", 2), ("own0", 4), ("own1", 4)]
         placed = first + second + after_scales + rounded
         places = {name: KIB * sum(size for other, size in placed[:i]) for i, (name, unused) in enumerate(placed)}
         places["draft0"] = places[first[0][0]]
         places["draft1"] = places[second[0][0]]
-        for k in range(4):
-            places["eta%d" % k] = places["wo_raw0"] + 2 * KIB * (k % 2)
+        for k in range(2):
+            places["eta%d" % k] = places["wo_raw00"] + 2 * KIB * k
+            places["eta%d" % (k + 2)] = places["own%d" % k]
+            places["scaled%d" % (k + 2)] = places["own%d" % k] + 2 * KIB
         places["gate"] = places["wa_raw1"]
-        places["picked04"] = places["wa0_bf0"]
+        places["picked06"] = places["wa0_bf0"]
         places["picked12"] = places["wa1_bf0"]
-        places["picked16"] = places["wo1_bf1"]
+        places["picked16"] = places["eta1"]
         places["page%d" % LAST_PAGE] = places["wo0_bf0"]
         for h in range(2):
             places["pairs%d" % h] = places["tab_w%d" % h]
@@ -92,17 +94,16 @@ def tile_list_rgg_ownP_kernel(
         drafts = [region("draft0", first, F32, 4)[:, 0:P], region("draft1", second, F32, 4)[:, 0:P]]
         ident = sb("ident", [P, P], F32)
         make_identity(nc, drafts[0])
+        src_s1 = sb("src_s1", [P, J], U8)
+        nc.gpsimd.memset(src_s1[:].bitcast(I32), 0)
         nc.vector.tensor_copy(drafts[1], drafts[0])
         wb_s = at_place("wb_s", [P, PASSES, N], U8)
         nc.vector.memset(wb_s[:].bitcast(I32), 0)
         gate_rows = at_place("gate_rows", [P, P], F32)
         nc.vector.memset(gate_rows[:], 0.0)
         nc.vector.tensor_copy(ident[:], drafts[1])
-        planes = [at_place(name, [P, J + 4], U8) for name in ("wc_s", "src_s1")]
-        for plane in planes:
-            nc.vector.memset(plane[:].bitcast(I32), 0)
-        wc_s = planes[0][:, 0:J].rearrange("p (a n) -> p a n", a=PASSES)
-        src_s1 = planes[1][:, 0:J]
+        wc_s = at_place("wc_s", [P, PASSES, N], U8)
+        nc.gpsimd.memset(wc_s[:].bitcast(I32), 0)
 
         pages = {}
 
@@ -113,8 +114,6 @@ def tile_list_rgg_ownP_kernel(
         for t in PAGE_ORDER[:3]:
             clear_page(t)
 
-        wb_w = sb("wb_w", [P, PASSES, 2 * N], U8)
-        nc.sync.dma_start(wb_w[:].bitcast(I32), wb_words.rearrange("a p b -> p a b").bitcast(I32))
         for q in range(QUADS):
             nc.sync.dma_start(tab_s[32 * q : 32 * q + 8, :].bitcast(I32), tab_scales[:, 4 * q : 4 * q + 4, :].bitcast(I32))
 
@@ -135,6 +134,8 @@ def tile_list_rgg_ownP_kernel(
             nc.sync.dma_start(words[:], tab_words[a].rearrange("p t i -> p (t i)").bitcast(I32))
             return words
 
+        wb_w = sb("wb_w", [P, PASSES, 2 * N], U8)
+        nc.sync.dma_start(wb_w[:].bitcast(I32), wb_words.rearrange("a p b -> p a b").bitcast(I32))
         tab_w = [load_table(0)]
         load_scales(wb_s, wb_scales)
         nc.sync.dma_start(gate_rows[0:TILES, :], wgo[0:1, :].rearrange("o (b c) -> (o b) c", c=P))
@@ -148,6 +149,9 @@ def tile_list_rgg_ownP_kernel(
         nc.tensor.transpose(gate_ps[:, 0:P], gate_rows[:], ident[:])
         gate = at_place("gate", [P, TILES], F32)
         nc.scalar.copy(gate[:], gate_ps[:, 0:TILES])
+
+        def gpsimd_round(out, in_):
+            nc.gpsimd.tensor_scalar(out, in_, 1.0, -0.0, MULT, ADD)
 
         picked = {}
 
@@ -176,19 +180,18 @@ def tile_list_rgg_ownP_kernel(
         nc.sync.dma_start(src_s1[0:SHIFT_ROWS, :].bitcast(I32), src_s[4 : 4 + SHIFT_ROWS, :].bitcast(I32))
         nc.vector.tensor_copy(dst_s[:], tab_s.indirect(dst_list[:]))
         tab_w.append(load_table(1))
-        wo_first = load_rows(wo, 0, "wo_raw0")
-        wo_second = [load_rows(wo, 1, "wo_raw%d" % (1 + h), slice(h * N // 2, (h + 1) * N // 2)) for h in range(2)]
+        wo_raw = [[load_rows(wo, 0, "wo_raw00")]]
+        wo_raw.append([load_rows(wo, 1, "wo_raw1%d" % h, slice(h * N // 2, (h + 1) * N // 2)) for h in range(2)])
         wc_w = at_place("wc_w", [P, PASSES, N], U32)
         nc.sync.dma_start(wc_w[:].bitcast(I32), wc_words.rearrange("a p n i -> p a (n i)").bitcast(I32))
-        gather_words(0, 0, 2)
-        gather_words(0, 2, 4)
+        gather_words(0, 0, 6)
         wa_q = [quantise_weight([wa_raw[0]], "wa0", [nc.scalar.copy])]
-        gather_words(0, 4, 8)
+        gather_words(0, 6, 8)
         wa_q.append(quantise_weight([wa_raw[1]], "wa1", [nc.scalar.copy]))
         gather_words(1, 0, 2)
         gather_words(1, 2, 6)
-        wo_q = [quantise_weight([wo_first], "wo0", [nc.scalar.copy])]
-        wo_q.append(quantise_weight(wo_second, "wo1", [nc.scalar.copy, nc.vector.tensor_copy]))
+        wo_q = [quantise_weight(wo_raw[0], "wo0", [nc.scalar.copy])]
+        wo_q.append(quantise_weight(wo_raw[1], "wo1", [nc.scalar.copy, nc.vector.tensor_copy]))
         clear_page(LAST_PAGE)
         wb_q = [(wb_w[:, a, :].bitcast(FP4X4), wb_s[:, a, :]) for a in range(PASSES)]
         wc_q = [(wc_w[:, a, :].bitcast(FP8X4), wc_s[:, a, :]) for a in range(PASSES)]
@@ -212,7 +215,7 @@ def tile_list_rgg_ownP_kernel(
         def dealt(acc):
             return acc[:].rearrange("p (m t) -> p t m", t=PACK)
 
-        msg, own = {}, {}
+        msg, own, sums = {}, {}, {}
 
         def message(k):
             za = bank(k if k < 4 else k % 2, "za%d" % k)
@@ -228,7 +231,7 @@ def tile_list_rgg_ownP_kernel(
             if k < 2:
                 nc.vector.scalar_tensor_tensor(msg[k][:], dealt(ms), gate[:, k : k + 1], eta[:], MULT, MULT)
             else:
-                scaled = sb("scaled%d" % k, [P, PACK, P], F32)
+                scaled = (at_place if k < 4 else sb)("scaled%d" % k, [P, PACK, P], F32)
                 nc.scalar.activation(scaled[:], dealt(ms), ACT.Copy, scale=gate[:, k : k + 1])
                 nc.gpsimd.tensor_tensor(msg[k][:], scaled[:], eta[:], MULT)
 
@@ -236,8 +239,18 @@ def tile_list_rgg_ownP_kernel(
             ow = bank(6 + k if k < 2 else 2 + k % 2, "ow%d" % k)
             for a in range(PASSES):
                 mx_pass(ow, k, DST, a, wo_q, a == 0, a == PASSES - 1)
-            own[k] = sb("own%d" % k, [P, PACK, P], F32)
-            nc.scalar.activation(own[k][:], dealt(ow), ACT.Copy, scale=gate[:, k : k + 1])
+            sums[k] = ow
+            if k < 2:
+                scale_own(k, 0, 2, at_place)
+            else:
+                scale_own(k, 0, 1, sb)
+
+        def scale_own(k, first, step, make):
+            part = make("own%d" % (k + TILES * first), [P, 2 * PACK if make is at_place else PACK // step, P], F32)
+            part = part[:, 0 : PACK // step, :]
+            nc.scalar.activation(part, dealt(sums[k])[:, first:PACK:step, :], ACT.Copy, scale=gate[:, k : k + 1])
+            for t in range(first, PACK, step):
+                own[k, t] = part[:, t // step, :]
 
         def place_results(b, pieces, tag=None):
             name = "%d%d" % pieces[0][0:2]
@@ -246,7 +259,7 @@ def tile_list_rgg_ownP_kernel(
             for t, first, last in pieces:
                 for k in range(first, last):
                     cols = acc[:, col : col + P]
-                    nc.tensor.matmul(cols, own[k][:, t, :], ident[:], start=True, stop=False, is_transpose=True)
+                    nc.tensor.matmul(cols, own[k, t], ident[:], start=True, stop=False, is_transpose=True)
                     nc.tensor.matmul(cols, msg[k][:, t, :], ident[:], start=False, stop=True, is_transpose=True)
                     col = col + P
             vals = sb("vals" + name, [P, col], F32, tag)
@@ -259,7 +272,7 @@ def tile_list_rgg_ownP_kernel(
 
         def place_pair(g, u):
             two_pages = PAGE_ORDER[2 * u : 2 * u + 2]
-            place_results(u if g == 0 else 6 + u, [(t, 2 * g, 2 * g + 2) for t in two_pages if g < PAIRS // 2 or t != LAST_PAGE])
+            place_results(0 if g == 0 else 6 + u, [(t, 2 * g, 2 * g + 2) for t in two_pages if g < PAIRS // 2 or t != LAST_PAGE])
 
         for k in range(2):
             message(k)
@@ -268,22 +281,28 @@ def tile_list_rgg_ownP_kernel(
             for k in (2 * g, 2 * g + 1):
                 projection(k)
             if g == 0:
-                place_pair(g, 0)
+                for u in range(2):
+                    place_results(u, [(PAGE_ORDER[u], 0, 2)])
+                for k in range(2):
+                    scale_own(k, 1, 2, sb)
+                place_pair(g, 1)
             for k in range(2 * g + 2, min(2 * g + 4, TILES)):
                 message(k)
             if g > 0:
                 place_pair(g, 0)
-            place_pair(g, 1)
+                place_pair(g, 1)
         place_results(4, [(LAST_PAGE, TILES // 2, TILES)], "vals%d%d" % (PAGE_ORDER[0], TILES - 2))
 
-        pairs = [at_place("pairs%d" % h, [P, 2, T // 2, 2], BF16) for h in range(2)]
+        pairs = [at_place("pairs%d" % h, [P, 2, 2, CHUNK, 2], BF16) for h in range(2)]
         out_rows = out_0.rearrange("(p t) c -> p t c", t=PACK)
 
-        def gpsimd_round(out, in_):
-            nc.gpsimd.tensor_scalar(out, in_, 1.0, -0.0, MULT, ADD)
-
         def round_page(t, h, copy):
-            copy(pairs[h][:, t // 2, :, t % 2], pages[t][:, h * T // 2 : (h + 1) * T // 2])
+            half = pages[t][:, h * T // 2 : (h + 1) * T // 2].rearrange("p (b c) -> p b c", b=2)
+            if t != LAST_PAGE:
+                copy(pairs[h][:, :, t // 2, :, t % 2], half)
+            else:
+                for b in range(2):
+                    copy(pairs[h][:, b, t // 2, :, t % 2], half[:, b, :])
 
         first_half_by = (gpsimd_round, gpsimd_round, nc.scalar.copy, nc.vector.tensor_copy)
         for t in PAGE_ORDER:
@@ -293,25 +312,27 @@ def tile_list_rgg_ownP_kernel(
 
         woven = [at_place("woven%d" % c, [P, CHUNK, 2], U32) for c in range(CHUNKS)]
 
-        def weave(c, copy, word):
-            words = pairs[c // 2][:].rearrange("p u c e -> p u (c e)").bitcast(word)
-            cols = slice(c % 2 * CHUNK, (c % 2 + 1) * CHUNK)
-            copy(woven[c][:].bitcast(word), words[:, :, cols].rearrange("p u c -> p c u"))
+        def weave(c, copy, word, cols):
+            words = pairs[c // 2][:, c % 2, :, :, :].rearrange("p u c e -> p u (c e)").bitcast(word)
+            copy(woven[c][:, cols, :].bitcast(word), words[:, :, cols].rearrange("p u c -> p c u"))
 
-        weave(CHUNKS - 1, nc.scalar.copy, U32)
-        for c in range(CHUNKS // 2):
-            weave(c, nc.vector.tensor_copy, I32)
+        pieces = [(c, slice(0, CHUNK)) for c in range(CHUNKS)]
+        for c, cols in pieces:
+            if c < CHUNKS // 2:
+                weave(c, nc.vector.tensor_copy, I32, cols)
+            else:
+                weave(c, nc.scalar.copy, U32, cols)
         out_s = sb("out_s", [P, T], U8)
         out_words = out_1[0].rearrange("p t i -> p (t i)").bitcast(I32)
-        for c in range(CHUNKS):
-            if c == CHUNKS // 2:
-                weave(c, nc.vector.tensor_copy, I32)
-            cols = slice(c * CHUNK, (c + 1) * CHUNK)
-            codes = sb("out_w%d" % c, [P, CHUNK], U32)
+        for c, cols in pieces:
+            place = slice(c * CHUNK + cols.start, c * CHUNK + cols.stop)
+            codes = sb("out_w%d" % place.start, [P, cols.stop - cols.start], U32)
             nc.vector.quantize_mx(
-                out=codes[:].bitcast(FP8X4), scales=out_s[:, cols], in_=woven[c][:].rearrange("p c u -> p (c u)").bitcast(BF16)
+                out=codes[:].bitcast(FP8X4),
+                scales=out_s[:, place],
+                in_=woven[c][:, cols, :].rearrange("p c u -> p (c u)").bitcast(BF16),
             )
-            nc.sync.dma_start(out_words[:, cols], codes[:].bitcast(I32))
+            nc.sync.dma_start(out_words[:, place], codes[:].bitcast(I32))
         for q in range(QUADS):
             queue = (nc.scalar, nc.sync)[q % 2]
             queue.dma_start(out_2[0, 4 * q : 4 * q + 4, :].bitcast(I32), out_s[32 * q : 32 * q + 4, :].bitcast(I32))

@@ -48,28 +48,27 @@ def tile_list_rgg_ownP_kernel(
         def sb(name, shape, dtype, tag=None):
             return keep.tile(shape, dtype, name=name, tag=tag or name, align_bytes=64)
 
-        first = [("tab_w0", 8), ("wb_s", 1), ("gate_rows", 1)]
-        second = [("wa_raw0", 8), ("wa_raw1", 8), ("wc_s", 1), ("src_s", 1), ("dst_s", 1)]
+        first = [("wa_raw0", 8), ("wb_s", 2), ("gate_rows", 1)]
+        second = [("tab_w0", 8), ("wa_raw1", 8), ("wc_s", 2), ("src_s1", 2), ("src_s", 1), ("dst_s", 1)]
         second = second + [("page%d" % t, 8) for t in PAGE_ORDER[:3]]
-        after_scales = [("tab_s", 2), ("tab_w1", 8), ("wo_raw00", 8), ("wo_raw10", 4), ("wo_raw11", 4), ("wc_w", 4)]
-        rounded = [("wa0_bf0", 4), ("wa1_bf0", 4), ("wo0_bf0", 4), ("wo1_bf0", 2), ("wo1_bf1", 2), ("own0", 4), ("own1", 4)]
+        after_scales = [("tab_s", 3), ("tab_w1", 8), ("wo_raw00", 4), ("wo_raw01", 4), ("wo_raw10", 4), ("wo_raw11", 4), ("wc_w", 4)]
+        rounded = [("wa0_bf0", 6), ("wa1_bf0", 4), ("wo0_bf0", 10), ("wo0_bf1", 2), ("wo1_bf0", 2), ("wo1_bf1", 2), ("own0", 4), ("own1", 4)]
         placed = first + second + after_scales + rounded
         places = {name: KIB * sum(size for other, size in placed[:i]) for i, (name, unused) in enumerate(placed)}
-        places["draft0"] = places[first[0][0]]
-        places["draft1"] = places[second[0][0]]
         for k in range(2):
-            places["eta%d" % k] = places["wo_raw00"] + 2 * KIB * k
+            places["eta%d" % k] = places["wo_raw10"] + 2 * KIB * k
             places["eta%d" % (k + 2)] = places["own%d" % k]
             places["scaled%d" % (k + 2)] = places["own%d" % k] + 2 * KIB
         places["gate"] = places["wa_raw1"]
-        places["picked06"] = places["wa0_bf0"]
-        places["picked12"] = places["wa1_bf0"]
-        places["picked16"] = places["eta1"]
-        places["page%d" % LAST_PAGE] = places["wo0_bf0"]
+        places["picked02"] = places["wa0_bf0"]
+        places["gate_first"] = places["wa_raw1"] + 2 * KIB
+        places["picked16"] = places["gate_first"]
+        places["picked14"] = places["wo0_bf1"]
+        places["page%d" % LAST_PAGE] = places["wo0_bf0"] + 2 * KIB
         for h in range(2):
             places["pairs%d" % h] = places["tab_w%d" % h]
         for c in range(CHUNKS):
-            places["woven%d" % c] = places["wa_raw0"] + 4 * KIB * c
+            places["woven%d" % c] = places["wa_raw%d" % (c // 2)] + 4 * KIB * (c % 2)
 
         def at_place(name, shape, dtype):
             return staged.tile(shape, dtype, name=name, tag=name, align_bytes=64, offset=places[name])
@@ -89,21 +88,19 @@ def tile_list_rgg_ownP_kernel(
         def region(name, parts, dtype, size):
             return at_place(name, [P, KIB * sum(kib for other, kib in parts) // size], dtype)
 
-        tab_s = region("tab_s", after_scales, U8, 1)[:, 0:T]
-        nc.vector.memset(tab_s.bitcast(I32), 0)
-        drafts = [region("draft0", first, F32, 4)[:, 0:P], region("draft1", second, F32, 4)[:, 0:P]]
+        def zeroed(tile, size):
+            nc.vector.memset(tile[:, 0 : size + 4].bitcast(I32), 0)
+            return tile[:, 0:size]
+
         ident = sb("ident", [P, P], F32)
-        make_identity(nc, drafts[0])
-        src_s1 = sb("src_s1", [P, J], U8)
-        nc.gpsimd.memset(src_s1[:].bitcast(I32), 0)
-        nc.vector.tensor_copy(drafts[1], drafts[0])
-        wb_s = at_place("wb_s", [P, PASSES, N], U8)
-        nc.vector.memset(wb_s[:].bitcast(I32), 0)
-        gate_rows = at_place("gate_rows", [P, P], F32)
+        make_identity(nc, ident[:])
+        tab_s = zeroed(region("tab_s", after_scales, U8, 1), T)
+        wb_s = zeroed(at_place("wb_s", [P, J + 4], U8), J).rearrange("p (a n) -> p a n", a=PASSES)
+        gate_rows = at_place("gate_rows", [P, P + 1], F32)
         nc.vector.memset(gate_rows[:], 0.0)
-        nc.vector.tensor_copy(ident[:], drafts[1])
-        wc_s = at_place("wc_s", [P, PASSES, N], U8)
-        nc.gpsimd.memset(wc_s[:].bitcast(I32), 0)
+        gate_rows = gate_rows[:, 0:P]
+        wc_s = zeroed(at_place("wc_s", [P, J + 4], U8), J).rearrange("p (a n) -> p a n", a=PASSES)
+        src_s1 = zeroed(at_place("src_s1", [P, J + 4], U8), J)
 
         pages = {}
 
@@ -114,6 +111,8 @@ def tile_list_rgg_ownP_kernel(
         for t in PAGE_ORDER[:3]:
             clear_page(t)
 
+        wb_w = sb("wb_w", [P, PASSES, 2 * N], U8)
+        nc.sync.dma_start(wb_w[:].bitcast(I32), wb_words.rearrange("a p b -> p a b").bitcast(I32))
         for q in range(QUADS):
             nc.sync.dma_start(tab_s[32 * q : 32 * q + 8, :].bitcast(I32), tab_scales[:, 4 * q : 4 * q + 4, :].bitcast(I32))
 
@@ -134,21 +133,22 @@ def tile_list_rgg_ownP_kernel(
             nc.sync.dma_start(words[:], tab_words[a].rearrange("p t i -> p (t i)").bitcast(I32))
             return words
 
-        wb_w = sb("wb_w", [P, PASSES, 2 * N], U8)
-        nc.sync.dma_start(wb_w[:].bitcast(I32), wb_words.rearrange("a p b -> p a b").bitcast(I32))
-        tab_w = [load_table(0)]
+        wa_raw = [load_rows(wa, 0, "wa_raw0")]
         load_scales(wb_s, wb_scales)
         nc.sync.dma_start(gate_rows[0:TILES, :], wgo[0:1, :].rearrange("o (b c) -> (o b) c", c=P))
-        wa_raw = [load_rows(wa, a, "wa_raw%d" % a) for a in range(PASSES)]
+        tab_w = [load_table(0)]
+        wa_raw.append(load_rows(wa, 1, "wa_raw1"))
         load_scales(wc_s, wc_scales)
 
         src_s = at_place("src_s", [P, J], U8)
         dst_s = at_place("dst_s", [P, J], U8)
 
         gate_ps = bank(7, "gate_ps")
-        nc.tensor.transpose(gate_ps[:, 0:P], gate_rows[:], ident[:])
+        nc.tensor.transpose(gate_ps[:, 0:P], gate_rows, ident[:])
         gate = at_place("gate", [P, TILES], F32)
         nc.scalar.copy(gate[:], gate_ps[:, 0:TILES])
+        gate_first = at_place("gate_first", [P, 2], F32)
+        nc.scalar.copy(gate_first[:], gate_ps[:, 0:2])
 
         def gpsimd_round(out, in_):
             nc.gpsimd.tensor_scalar(out, in_, 1.0, -0.0, MULT, ADD)
@@ -163,36 +163,39 @@ def tile_list_rgg_ownP_kernel(
             for k in range(first, last):
                 picked[a, k] = words[:, :, (k - first) * P : (k - first + 1) * P]
 
-        def quantise_weight(raws, name, copies):
+        def quantise_weight(raws, name, copies, spare=0):
             codes = sb(name + "_codes", [P, N], U32)
             scales = sb(name + "_scales", [P, N], U8)
             width = N // len(raws)
             for j, raw in enumerate(raws):
                 cols = slice(j * width, (j + 1) * width)
-                grouped = at_place("%s_bf%d" % (name, j), [P, width, PACK], BF16)
-                copies[j](grouped[:].rearrange("p (c e) i -> p c i e", e=4), raw[:].rearrange("p i (c e) -> p c i e", e=4))
+                grouped = at_place("%s_bf%d" % (name, j), [P, width + spare * (1 - j), PACK], BF16)[:, 0:width, :]
+                copies[j](grouped.rearrange("p (c e) i -> p c i e", e=4), raw[:].rearrange("p i (c e) -> p c i e", e=4))
                 nc.vector.quantize_mx(
-                    out=codes[:, cols].bitcast(FP8X4), scales=scales[:, cols], in_=grouped[:].rearrange("p n i -> p (n i)")
+                    out=codes[:, cols].bitcast(FP8X4), scales=scales[:, cols], in_=grouped.rearrange("p n i -> p (n i)")
                 )
             return codes[:].bitcast(FP8X4), scales[:]
 
         nc.vector.tensor_copy(src_s[:], tab_s.indirect(src_list[:]))
         nc.sync.dma_start(src_s1[0:SHIFT_ROWS, :].bitcast(I32), src_s[4 : 4 + SHIFT_ROWS, :].bitcast(I32))
         nc.vector.tensor_copy(dst_s[:], tab_s.indirect(dst_list[:]))
+        halves = [slice(h * N // 2, (h + 1) * N // 2) for h in range(2)]
+        wo_raw = [[load_rows(wo, 0, "wo_raw00", halves[0])]]
         tab_w.append(load_table(1))
-        wo_raw = [[load_rows(wo, 0, "wo_raw00")]]
-        wo_raw.append([load_rows(wo, 1, "wo_raw1%d" % h, slice(h * N // 2, (h + 1) * N // 2)) for h in range(2)])
+        wo_raw[0].append(load_rows(wo, 0, "wo_raw01", halves[1]))
+        wo_raw.append([load_rows(wo, 1, "wo_raw1%d" % h, halves[h]) for h in range(2)])
         wc_w = at_place("wc_w", [P, PASSES, N], U32)
         nc.sync.dma_start(wc_w[:].bitcast(I32), wc_words.rearrange("a p n i -> p a (n i)").bitcast(I32))
-        gather_words(0, 0, 6)
+        gather_words(0, 0, 2)
         wa_q = [quantise_weight([wa_raw[0]], "wa0", [nc.scalar.copy])]
-        gather_words(0, 6, 8)
+        gather_words(0, 2, 8)
         wa_q.append(quantise_weight([wa_raw[1]], "wa1", [nc.scalar.copy]))
         gather_words(1, 0, 2)
-        gather_words(1, 2, 6)
-        wo_q = [quantise_weight(wo_raw[0], "wo0", [nc.scalar.copy])]
-        wo_q.append(quantise_weight(wo_raw[1], "wo1", [nc.scalar.copy, nc.vector.tensor_copy]))
+        gather_words(1, 2, 4)
+        wo_q = [quantise_weight(wo_raw[0], "wo0", [nc.scalar.copy, nc.scalar.copy], 2 * N)]
         clear_page(LAST_PAGE)
+        gather_words(1, 4, 6)
+        wo_q.append(quantise_weight(wo_raw[1], "wo1", [nc.scalar.copy, nc.vector.tensor_copy]))
         wb_q = [(wb_w[:, a, :].bitcast(FP4X4), wb_s[:, a, :]) for a in range(PASSES)]
         wc_q = [(wc_w[:, a, :].bitcast(FP8X4), wc_s[:, a, :]) for a in range(PASSES)]
 
@@ -215,7 +218,7 @@ def tile_list_rgg_ownP_kernel(
         def dealt(acc):
             return acc[:].rearrange("p (m t) -> p t m", t=PACK)
 
-        msg, own, sums = {}, {}, {}
+        msg, own, sums, later = {}, {}, {}, []
 
         def message(k):
             za = bank(k if k < 4 else k % 2, "za%d" % k)
@@ -229,7 +232,11 @@ def tile_list_rgg_ownP_kernel(
                 mx_pass(ms, k, SRC, a, wc_q, a == 0, a == PASSES - 1)
             msg[k] = sb("msg%d" % k, [P, PACK, P], F32)
             if k < 2:
-                nc.vector.scalar_tensor_tensor(msg[k][:], dealt(ms), gate[:, k : k + 1], eta[:], MULT, MULT)
+                even = slice(0, PACK, 2)
+                nc.vector.scalar_tensor_tensor(
+                    msg[k][:, even, :], dealt(ms)[:, even, :], gate_first[:, k : k + 1], eta[:, even, :], MULT, MULT
+                )
+                later.append((k, ms, eta))
             else:
                 scaled = (at_place if k < 4 else sb)("scaled%d" % k, [P, PACK, P], F32)
                 nc.scalar.activation(scaled[:], dealt(ms), ACT.Copy, scale=gate[:, k : k + 1])
@@ -283,6 +290,10 @@ def tile_list_rgg_ownP_kernel(
             if g == 0:
                 for u in range(2):
                     place_results(u, [(PAGE_ORDER[u], 0, 2)])
+                for k, ms, eta in later:
+                    scaled = sb("scaled%d" % k, [P, PACK // 2, P], F32)
+                    nc.scalar.activation(scaled[:], dealt(ms)[:, 1:PACK:2, :], ACT.Copy, scale=gate[:, k : k + 1])
+                    nc.gpsimd.tensor_tensor(msg[k][:, 1:PACK:2, :], scaled[:], eta[:, 1:PACK:2, :], MULT)
                 for k in range(2):
                     scale_own(k, 1, 2, sb)
                 place_pair(g, 1)

@@ -28,10 +28,9 @@ GROUP = 16
 CHUNK = 512
 CHUNKS = T // CHUNK
 SRC, DST = 0, 1
-SHIFT_ROWS = 3 * 32 + 4
 KIB = 1024
 
-PAGE_ORDER = (2, 0, 1, 3)
+PAGE_ORDER = (0, 2, 1, 3)
 LAST_PAGE = PAGE_ORDER[-1]
 
 
@@ -49,12 +48,13 @@ def tile_list_rgg_ownP_kernel(
             return keep.tile(shape, dtype, name=name, tag=tag or name, align_bytes=64)
 
         first = [("wa_raw0", 8), ("wb_s", 2), ("gate_rows", 1)]
-        second = [("tab_w0", 8), ("wa_raw1", 8), ("wc_s", 2), ("src_s1", 2), ("src_s", 1), ("dst_s", 1)]
-        second = second + [("page%d" % t, 8) for t in PAGE_ORDER[:3]]
+        second = [("tab_w0", 8), ("wa_raw1", 8), ("wc_s", 2), ("src_s1", 2)]
+        cleared = [("page%d" % t, 8) for t in PAGE_ORDER[:3]] + [("src_s", 1), ("dst_s", 1)]
         after_scales = [("tab_s", 3), ("tab_w1", 8), ("wo_raw00", 4), ("wo_raw01", 4), ("wo_raw10", 4), ("wo_raw11", 4), ("wc_w", 4)]
         rounded = [("wa0_bf0", 6), ("wa1_bf0", 4), ("wo0_bf0", 10), ("wo0_bf1", 2), ("wo1_bf0", 2), ("wo1_bf1", 2), ("own0", 4), ("own1", 4)]
-        placed = first + second + after_scales + rounded
+        placed = first + second + cleared + after_scales + rounded
         places = {name: KIB * sum(size for other, size in placed[:i]) for i, (name, unused) in enumerate(placed)}
+        places["draft"] = places[cleared[0][0]]
         for k in range(2):
             places["eta%d" % k] = places["wo_raw10"] + 2 * KIB * k
             places["eta%d" % (k + 2)] = places["own%d" % k]
@@ -89,18 +89,19 @@ def tile_list_rgg_ownP_kernel(
             return at_place(name, [P, KIB * sum(kib for other, kib in parts) // size], dtype)
 
         def zeroed(tile, size):
-            nc.vector.memset(tile[:, 0 : size + 4].bitcast(I32), 0)
+            nc.vector.memset(tile[:, 0:size].bitcast(I32), 0)
             return tile[:, 0:size]
 
-        ident = sb("ident", [P, P], F32)
-        make_identity(nc, ident[:])
+        draft = region("draft", cleared, F32, 4)[:, 0:P]
+        make_identity(nc, draft)
         tab_s = zeroed(region("tab_s", after_scales, U8, 1), T)
-        wb_s = zeroed(at_place("wb_s", [P, J + 4], U8), J).rearrange("p (a n) -> p a n", a=PASSES)
-        gate_rows = at_place("gate_rows", [P, P + 1], F32)
-        nc.vector.memset(gate_rows[:], 0.0)
-        gate_rows = gate_rows[:, 0:P]
-        wc_s = zeroed(at_place("wc_s", [P, J + 4], U8), J).rearrange("p (a n) -> p a n", a=PASSES)
-        src_s1 = zeroed(at_place("src_s1", [P, J + 4], U8), J)
+        wb_s = zeroed(at_place("wb_s", [P, J], U8), J).rearrange("p (a n) -> p a n", a=PASSES)
+        gate_rows = at_place("gate_rows", [P, P], F32)[:]
+        nc.vector.memset(gate_rows, 0.0)
+        wc_s = zeroed(at_place("wc_s", [P, J], U8), J).rearrange("p (a n) -> p a n", a=PASSES)
+        src_s1 = zeroed(at_place("src_s1", [P, J], U8), J)
+        ident = sb("ident", [P, P], F32)
+        nc.vector.tensor_copy(ident[:], draft)
 
         pages = {}
 
@@ -137,8 +138,8 @@ def tile_list_rgg_ownP_kernel(
         load_scales(wb_s, wb_scales)
         nc.sync.dma_start(gate_rows[0:TILES, :], wgo[0:1, :].rearrange("o (b c) -> (o b) c", c=P))
         tab_w = [load_table(0)]
-        wa_raw.append(load_rows(wa, 1, "wa_raw1"))
         load_scales(wc_s, wc_scales)
+        wa_raw.append(load_rows(wa, 1, "wa_raw1"))
 
         src_s = at_place("src_s", [P, J], U8)
         dst_s = at_place("dst_s", [P, J], U8)
@@ -177,7 +178,8 @@ def tile_list_rgg_ownP_kernel(
             return codes[:].bitcast(FP8X4), scales[:]
 
         nc.vector.tensor_copy(src_s[:], tab_s.indirect(src_list[:]))
-        nc.sync.dma_start(src_s1[0:SHIFT_ROWS, :].bitcast(I32), src_s[4 : 4 + SHIFT_ROWS, :].bitcast(I32))
+        for q in range(QUADS):
+            nc.sync.dma_start(src_s1[32 * q : 32 * q + 4, :].bitcast(I32), src_s[32 * q + 4 : 32 * q + 8, :].bitcast(I32))
         nc.vector.tensor_copy(dst_s[:], tab_s.indirect(dst_list[:]))
         halves = [slice(h * N // 2, (h + 1) * N // 2) for h in range(2)]
         wo_raw = [[load_rows(wo, 0, "wo_raw00", halves[0])]]
@@ -302,24 +304,29 @@ def tile_list_rgg_ownP_kernel(
             if g > 0:
                 place_pair(g, 0)
                 place_pair(g, 1)
-        place_results(4, [(LAST_PAGE, TILES // 2, TILES)], "vals%d%d" % (PAGE_ORDER[0], TILES - 2))
+        place_results(4, [(LAST_PAGE, TILES // 2, TILES)])
 
         pairs = [at_place("pairs%d" % h, [P, 2, 2, CHUNK, 2], BF16) for h in range(2)]
         out_rows = out_0.rearrange("(p t) c -> p t c", t=PACK)
 
-        def round_page(t, h, copy):
-            half = pages[t][:, h * T // 2 : (h + 1) * T // 2].rearrange("p (b c) -> p b c", b=2)
-            if t != LAST_PAGE:
-                copy(pairs[h][:, :, t // 2, :, t % 2], half)
-            else:
-                for b in range(2):
-                    copy(pairs[h][:, b, t // 2, :, t % 2], half[:, b, :])
+        def round_page(t, first, last, copy):
+            values = pages[t][:, first * CHUNK : last * CHUNK].rearrange("p (b c) -> p b c", c=CHUNK)
+            h = first // 2
+            copy(pairs[h][:, first - 2 * h : last - 2 * h, t // 2, :, t % 2], values)
 
-        first_half_by = (gpsimd_round, gpsimd_round, nc.scalar.copy, nc.vector.tensor_copy)
         for t in PAGE_ORDER:
             nc.sync.dma_start(out_rows[:, t, :], pages[t][:])
-            round_page(t, 0, first_half_by[t])
-            round_page(t, 1, nc.scalar.copy)
+            if t < 2:
+                round_page(t, 0, 2, gpsimd_round)
+                round_page(t, 2, 3, gpsimd_round)
+                round_page(t, 3, 4, nc.scalar.copy)
+            elif t == 2:
+                both = pages[t][:, 0 : T // 2].rearrange("p (b c) -> p b c", c=CHUNK).unsqueeze(3).to_broadcast([P, 2, CHUNK, 2])
+                nc.scalar.copy(pairs[0][:, :, 1, :, :], both)
+                round_page(t, 2, 4, nc.scalar.copy)
+            else:
+                for c in range(CHUNKS):
+                    round_page(t, c, c + 1, nc.vector.tensor_copy if c < 2 else nc.scalar.copy)
 
         woven = [at_place("woven%d" % c, [P, CHUNK, 2], U32) for c in range(CHUNKS)]
 

@@ -50,15 +50,16 @@ def tile_list_rgg_ownP_kernel(
         first = [("wa_raw0", 8), ("wb_s", 2), ("gate_rows", 1)]
         second = [("tab_w0", 8), ("wa_raw1", 8), ("wc_s", 2), ("src_s1", 2)]
         cleared = [("page%d" % t, 8) for t in PAGE_ORDER[:3]] + [("src_s", 1), ("dst_s", 1)]
-        after_scales = [("tab_s", 3), ("tab_w1", 8), ("wo_raw00", 4), ("wo_raw01", 4), ("wo_raw10", 4), ("wo_raw11", 4), ("wc_w", 4)]
+        after_scales = [("tab_s", 3), ("tab_w1", 8), ("wo_raw00", 4), ("wo_raw01", 4), ("wo_raw10", 6), ("wo_raw11", 4), ("wc_w", 4)]
         rounded = [("wa0_bf0", 6), ("wa1_bf0", 4), ("wo0_bf0", 10), ("wo0_bf1", 2), ("wo1_bf0", 2), ("wo1_bf1", 2), ("own0", 4), ("own1", 4)]
         placed = first + second + cleared + after_scales + rounded
         places = {name: KIB * sum(size for other, size in placed[:i]) for i, (name, unused) in enumerate(placed)}
         places["draft"] = places[cleared[0][0]]
         for k in range(2):
             places["eta%d" % k] = places["wo_raw10"] + 2 * KIB * k
-            places["eta%d" % (k + 2)] = places["own%d" % k]
             places["scaled%d" % (k + 2)] = places["own%d" % k] + 2 * KIB
+        places["eta2"] = places["wo_raw10"] + 4 * KIB
+        places["eta3"] = places["own1"]
         places["gate"] = places["wa_raw1"]
         places["picked02"] = places["wa0_bf0"]
         places["gate_first"] = places["wa_raw1"] + 2 * KIB
@@ -124,9 +125,9 @@ def tile_list_rgg_ownP_kernel(
                     scales[:, 4 * q : 4 * q + 4, :].rearrange("a r n -> r a n").bitcast(I32),
                 )
 
-        def load_rows(w, a, name, cols=slice(0, N)):
-            raw = at_place(name, [P, PACK, cols.stop - cols.start], F32)
-            nc.sync.dma_start(raw[:], w[a * P * PACK : (a + 1) * P * PACK, cols].rearrange("(p i) n -> p i n", i=PACK))
+        def load_rows(w, a, name, cols=slice(0, N), spare=0):
+            raw = at_place(name, [P, PACK + spare, cols.stop - cols.start], F32)[:, 0:PACK, :]
+            nc.sync.dma_start(raw, w[a * P * PACK : (a + 1) * P * PACK, cols].rearrange("(p i) n -> p i n", i=PACK))
             return raw
 
         def load_table(a):
@@ -171,7 +172,7 @@ def tile_list_rgg_ownP_kernel(
             for j, raw in enumerate(raws):
                 cols = slice(j * width, (j + 1) * width)
                 grouped = at_place("%s_bf%d" % (name, j), [P, width + spare * (1 - j), PACK], BF16)[:, 0:width, :]
-                copies[j](grouped.rearrange("p (c e) i -> p c i e", e=4), raw[:].rearrange("p i (c e) -> p c i e", e=4))
+                copies[j](grouped.rearrange("p (c e) i -> p c i e", e=4), raw.rearrange("p i (c e) -> p c i e", e=4))
                 nc.vector.quantize_mx(
                     out=codes[:, cols].bitcast(FP8X4), scales=scales[:, cols], in_=grouped.rearrange("p n i -> p (n i)")
                 )
@@ -185,7 +186,7 @@ def tile_list_rgg_ownP_kernel(
         wo_raw = [[load_rows(wo, 0, "wo_raw00", halves[0])]]
         tab_w.append(load_table(1))
         wo_raw[0].append(load_rows(wo, 0, "wo_raw01", halves[1]))
-        wo_raw.append([load_rows(wo, 1, "wo_raw1%d" % h, halves[h]) for h in range(2)])
+        wo_raw.append([load_rows(wo, 1, "wo_raw1%d" % h, halves[h], 2 - 2 * h) for h in range(2)])
         wc_w = at_place("wc_w", [P, PASSES, N], U32)
         nc.sync.dma_start(wc_w[:].bitcast(I32), wc_words.rearrange("a p n i -> p a (n i)").bitcast(I32))
         gather_words(0, 0, 2)
@@ -220,15 +221,19 @@ def tile_list_rgg_ownP_kernel(
         def dealt(acc):
             return acc[:].rearrange("p (m t) -> p t m", t=PACK)
 
-        msg, own, sums, later = {}, {}, {}, []
+        msg, own, sums, etas, later = {}, {}, {}, {}, []
 
-        def message(k):
+        def gating(k):
             za = bank(k if k < 4 else k % 2, "za%d" % k)
             for a in range(PASSES):
                 mx_pass(za, k, DST, a, wa_q, a == 0, False)
                 mx_pass(za, k, SRC, a, wb_q, False, a == PASSES - 1)
             eta = (at_place if k < 4 else sb)("eta%d" % k, [P, PACK, P], F32)
             nc.scalar.activation(eta[:], dealt(za), ACT.Sigmoid)
+            etas[k] = eta
+
+        def message(k):
+            eta = etas[k]
             ms = bank(4 + k % 2, "ms%d" % k)
             for a in range(PASSES):
                 mx_pass(ms, k, SRC, a, wc_q, a == 0, a == PASSES - 1)
@@ -284,26 +289,37 @@ def tile_list_rgg_ownP_kernel(
             place_results(0 if g == 0 else 6 + u, [(t, 2 * g, 2 * g + 2) for t in two_pages if g < PAIRS // 2 or t != LAST_PAGE])
 
         for k in range(2):
+            gating(k)
             message(k)
         gather_words(1, 6, 8)
-        for g in range(PAIRS):
-            for k in (2 * g, 2 * g + 1):
-                projection(k)
-            if g == 0:
-                for u in range(2):
-                    place_results(u, [(PAGE_ORDER[u], 0, 2)])
-                for k, ms, eta in later:
-                    scaled = sb("scaled%d" % k, [P, PACK // 2, P], F32)
-                    nc.scalar.activation(scaled[:], dealt(ms)[:, 1:PACK:2, :], ACT.Copy, scale=gate[:, k : k + 1])
-                    nc.gpsimd.tensor_tensor(msg[k][:, 1:PACK:2, :], scaled[:], eta[:, 1:PACK:2, :], MULT)
-                for k in range(2):
-                    scale_own(k, 1, 2, sb)
-                place_pair(g, 1)
-            for k in range(2 * g + 2, min(2 * g + 4, TILES)):
+        for k in range(2):
+            projection(k)
+        for u in range(2):
+            place_results(u, [(PAGE_ORDER[u], 0, 2)])
+        for k, ms, eta in later:
+            scaled = sb("scaled%d" % k, [P, PACK // 2, P], F32)
+            nc.scalar.activation(scaled[:], dealt(ms)[:, 1:PACK:2, :], ACT.Copy, scale=gate[:, k : k + 1])
+            nc.gpsimd.tensor_tensor(msg[k][:, 1:PACK:2, :], scaled[:], eta[:, 1:PACK:2, :], MULT)
+        for k in range(2):
+            scale_own(k, 1, 2, sb)
+        place_pair(0, 1)
+        for k in range(2, 4):
+            gating(k)
+            message(k)
+        for k in range(2, 4):
+            projection(k)
+        for k in range(4, 6):
+            gating(k)
+        for g in range(1, PAIRS):
+            ahead = range(2 * g + 2, min(2 * g + 4, TILES))
+            place_pair(g, 0)
+            for k in ahead:
                 message(k)
-            if g > 0:
-                place_pair(g, 0)
-                place_pair(g, 1)
+            place_pair(g, 1)
+            for k in ahead:
+                projection(k)
+            for k in range(2 * g + 4, min(2 * g + 6, TILES)):
+                gating(k)
         place_results(4, [(LAST_PAGE, TILES // 2, TILES)])
 
         pairs = [at_place("pairs%d" % h, [P, 2, 2, CHUNK, 2], BF16) for h in range(2)]

@@ -83,6 +83,11 @@ def tile_list_rgg_ownP_kernel(
         nc.sync.dma_start(dst_list[:], offs2)
         both_lists = (src_list, dst_list)
 
+        warm_in = sb("warm_in", [P, 1], F32)
+        nc.gpsimd.memset(warm_in[:], 0.0)
+        warm = sb("warm", [P, 1], F32)
+        nc.scalar.activation(warm[:], warm_in[:], ACT.Sigmoid)
+
         def entries(lst, first, last):
             return lst[:, first * P // GROUP : last * P // GROUP]
 

@@ -51,7 +51,7 @@ def tile_list_rgg_ownP_kernel(
         second = [("tab_w0", 8), ("wa_raw1", 8), ("wc_s", 2), ("src_s1", 2)]
         cleared = [("page%d" % t, 8) for t in PAGE_ORDER[:3]] + [("src_s", 1), ("dst_s", 1)]
         after_scales = [("tab_s", 3), ("tab_w1", 8), ("wo_raw00", 4), ("wo_raw01", 4), ("wo_raw10", 6), ("wo_raw11", 4), ("wc_w", 4)]
-        rounded = [("wa0_bf0", 6), ("wa1_bf0", 4), ("wo0_bf0", 10), ("wo0_bf1", 2), ("wo1_bf0", 2), ("wo1_bf1", 2), ("own0", 4), ("own1", 4)]
+        rounded = [("wa0_bf0", 14), ("wa1_bf0", 4), ("wo0_bf0", 2), ("wo0_bf1", 2), ("wo1_bf0", 2), ("wo1_bf1", 2), ("own0", 4), ("own1", 4)]
         placed = first + second + cleared + after_scales + rounded
         places = {name: KIB * sum(size for other, size in placed[:i]) for i, (name, unused) in enumerate(placed)}
         places["draft"] = places[cleared[0][0]]
@@ -65,7 +65,7 @@ def tile_list_rgg_ownP_kernel(
         places["gate_first"] = places["wa_raw1"] + 2 * KIB
         places["picked16"] = places["gate_first"]
         places["picked14"] = places["wo0_bf1"]
-        places["page%d" % LAST_PAGE] = places["wo0_bf0"] + 2 * KIB
+        places["page%d" % LAST_PAGE] = places["wa0_bf0"] + 6 * KIB
         for h in range(2):
             places["pairs%d" % h] = places["tab_w%d" % h]
         for c in range(CHUNKS):
@@ -195,13 +195,13 @@ def tile_list_rgg_ownP_kernel(
         wc_w = at_place("wc_w", [P, PASSES, N], U32)
         nc.sync.dma_start(wc_w[:].bitcast(I32), wc_words.rearrange("a p n i -> p a (n i)").bitcast(I32))
         gather_words(0, 0, 2)
-        wa_q = [quantise_weight([wa_raw[0]], "wa0", [nc.scalar.copy])]
+        wa_q = [quantise_weight([wa_raw[0]], "wa0", [nc.scalar.copy], N)]
+        clear_page(LAST_PAGE)
         gather_words(0, 2, 8)
         wa_q.append(quantise_weight([wa_raw[1]], "wa1", [nc.scalar.copy]))
         gather_words(1, 0, 2)
         gather_words(1, 2, 4)
-        wo_q = [quantise_weight(wo_raw[0], "wo0", [nc.scalar.copy, nc.scalar.copy], 2 * N)]
-        clear_page(LAST_PAGE)
+        wo_q = [quantise_weight(wo_raw[0], "wo0", [nc.scalar.copy, nc.scalar.copy])]
         gather_words(1, 4, 6)
         wo_q.append(quantise_weight(wo_raw[1], "wo1", [nc.scalar.copy, nc.vector.tensor_copy]))
         wb_q = [(wb_w[:, a, :].bitcast(FP4X4), wb_s[:, a, :]) for a in range(PASSES)]

@@ -64,6 +64,7 @@ def tile_list_rgg_ownP_kernel(
         places["picked02"] = places["wa0_bf0"]
         places["gate_first"] = places["wa_raw1"] + 2 * KIB
         places["picked16"] = places["gate_first"]
+        places["picked14s"] = places["gate_first"] + KIB
         places["picked14"] = places["wo0_bf1"]
         places["page%d" % LAST_PAGE] = places["wa0_bf0"] + 6 * KIB
         for h in range(2):
@@ -154,21 +155,21 @@ def tile_list_rgg_ownP_kernel(
         nc.tensor.transpose(gate_ps[:, 0:P], gate_rows, ident[:])
         gate = at_place("gate", [P, TILES], F32)
         nc.scalar.copy(gate[:], gate_ps[:, 0:TILES])
-        gate_first = at_place("gate_first", [P, 2], F32)
-        nc.scalar.copy(gate_first[:], gate_ps[:, 0:2])
+        gate_first = at_place("gate_first", [P, N], F32)[:, 0:2]
+        nc.scalar.copy(gate_first, gate_ps[:, 0:2])
 
         def gpsimd_round(out, in_):
             nc.gpsimd.tensor_scalar(out, in_, 1.0, -0.0, MULT, ADD)
 
         picked = {}
 
-        def gather_words(a, first, last):
-            name, shape = "picked%d%d" % (a, first), [P, 2, (last - first) * P]
+        def gather_words(a, first, last, sides=(DST, SRC), mark=""):
+            name, shape = "picked%d%d%s" % (a, first, mark), [P, len(sides), (last - first) * P]
             words = (at_place if name in places else sb)(name, shape, U32)
-            for s in (DST, SRC):
-                nc.vector.tensor_copy(words[:, s, :], tab_w[a][:].bitcast(U32).indirect(entries(both_lists[s], first, last)))
-            for k in range(first, last):
-                picked[a, k] = words[:, :, (k - first) * P : (k - first + 1) * P]
+            for i, s in enumerate(sides):
+                nc.vector.tensor_copy(words[:, i, :], tab_w[a][:].bitcast(U32).indirect(entries(both_lists[s], first, last)))
+                for k in range(first, last):
+                    picked[a, k, s] = words[:, i, (k - first) * P : (k - first + 1) * P]
 
         def quantise_weight(raws, name, copies, spare=0):
             codes = sb(name + "_codes", [P, N], U32)
@@ -202,7 +203,7 @@ def tile_list_rgg_ownP_kernel(
         gather_words(1, 0, 2)
         gather_words(1, 2, 4)
         wo_q = [quantise_weight(wo_raw[0], "wo0", [nc.scalar.copy, nc.scalar.copy])]
-        gather_words(1, 4, 6)
+        gather_words(1, 4, 6, (DST,))
         wo_q.append(quantise_weight(wo_raw[1], "wo1", [nc.scalar.copy, nc.vector.tensor_copy]))
         wb_q = [(wb_w[:, a, :].bitcast(FP4X4), wb_s[:, a, :]) for a in range(PASSES)]
         wc_q = [(wc_w[:, a, :].bitcast(FP8X4), wc_s[:, a, :]) for a in range(PASSES)]
@@ -215,7 +216,7 @@ def tile_list_rgg_ownP_kernel(
                 plane = (src_s, dst_s)[s][4 * a : P, cols]
             nc.tensor.matmul_mx(
                 out=acc[:],
-                lhsT=picked[a, k][:, s, :].bitcast(FP8X4),
+                lhsT=picked[a, k, s].bitcast(FP8X4),
                 lhsT_scale=plane,
                 rhs=weight[a][0],
                 rhs_scale=weight[a][1],
@@ -296,7 +297,8 @@ def tile_list_rgg_ownP_kernel(
         for k in range(2):
             gating(k)
             message(k)
-        gather_words(1, 6, 8)
+        gather_words(1, 4, 8, (SRC,), "s")
+        gather_words(1, 6, 8, (DST,))
         for k in range(2):
             projection(k)
         for u in range(2):

@@ -65,7 +65,7 @@ def tile_list_rgg_ownP_kernel(
         places["gate_first"] = places["wa_raw1"] + 2 * KIB
         places["picked16"] = places["gate_first"]
         places["picked14s"] = places["gate_first"] + KIB
-        places["picked14"] = places["wo0_bf1"]
+        places["picked14"] = places["wo1_bf1"]
         places["page%d" % LAST_PAGE] = places["wa0_bf0"] + 6 * KIB
         for h in range(2):
             places["pairs%d" % h] = places["tab_w%d" % h]
@@ -203,8 +203,8 @@ def tile_list_rgg_ownP_kernel(
         gather_words(1, 0, 2)
         gather_words(1, 2, 4)
         wo_q = [quantise_weight(wo_raw[0], "wo0", [nc.scalar.copy, nc.scalar.copy])]
-        gather_words(1, 4, 6, (DST,))
         wo_q.append(quantise_weight(wo_raw[1], "wo1", [nc.scalar.copy, nc.vector.tensor_copy]))
+        gather_words(1, 4, 6, (DST,))
         wb_q = [(wb_w[:, a, :].bitcast(FP4X4), wb_s[:, a, :]) for a in range(PASSES)]
         wc_q = [(wc_w[:, a, :].bitcast(FP8X4), wc_s[:, a, :]) for a in range(PASSES)]
 

@@ -125,10 +125,9 @@ def tile_list_rgg_ownP_kernel(
             nc.sync.dma_start(tab_s[32 * q : 32 * q + 8, :].bitcast(I32), tab_scales[:, 4 * q : 4 * q + 4, :].bitcast(I32))
 
         def load_scales(plane, scales):
-            for q in range(QUADS):
+            for r in range(4):
                 nc.sync.dma_start(
-                    plane[32 * q : 32 * q + 4, :, :].bitcast(I32),
-                    scales[:, 4 * q : 4 * q + 4, :].rearrange("a r n -> r a n").bitcast(I32),
+                    plane[r:P:32, :, :].bitcast(I32), scales[:, r:16:4, :].rearrange("a q n -> q a n").bitcast(I32)
                 )
 
         def load_rows(w, a, name, cols=slice(0, N), spare=0):
@@ -185,8 +184,8 @@ def tile_list_rgg_ownP_kernel(
             return codes[:].bitcast(FP8X4), scales[:]
 
         nc.vector.tensor_copy(src_s[:], tab_s.indirect(src_list[:]))
-        for q in range(QUADS):
-            nc.sync.dma_start(src_s1[32 * q : 32 * q + 4, :].bitcast(I32), src_s[32 * q + 4 : 32 * q + 8, :].bitcast(I32))
+        for r in range(4):
+            nc.sync.dma_start(src_s1[r:P:32, :].bitcast(I32), src_s[4 + r : P : 32, :].bitcast(I32))
         nc.vector.tensor_copy(dst_s[:], tab_s.indirect(dst_list[:]))
         halves = [slice(h * N // 2, (h + 1) * N // 2) for h in range(2)]
         wo_raw = [[load_rows(wo, 0, "wo_raw00", halves[0])]]
@@ -374,6 +373,6 @@ def tile_list_rgg_ownP_kernel(
                 in_=woven[c][:, cols, :].rearrange("p c u -> p (c u)").bitcast(BF16),
             )
             nc.sync.dma_start(out_words[:, place], codes[:].bitcast(I32))
-        for q in range(QUADS):
-            queue = (nc.scalar, nc.sync)[q % 2]
-            queue.dma_start(out_2[0, 4 * q : 4 * q + 4, :].bitcast(I32), out_s[32 * q : 32 * q + 4, :].bitcast(I32))
+        for r in range(4):
+            queue = (nc.scalar, nc.sync)[r % 2]
+            queue.dma_start(out_2[0, r:16:4, :].bitcast(I32), out_s[r:P:32, :].bitcast(I32))

@@ -101,7 +101,7 @@ def tile_list_rgg_ownP_kernel(
 
         draft = region("draft", cleared, F32, 4)[:, 0:P]
         make_identity(nc, draft)
-        tab_s = zeroed(region("tab_s", after_scales, U8, 1), T)
+        tab_s = zeroed(at_place("tab_s", [P, T], U8), T)
         wb_s = zeroed(at_place("wb_s", [P, J], U8), J).rearrange("p (a n) -> p a n", a=PASSES)
         gate_rows = at_place("gate_rows", [P, P], F32)[:]
         nc.vector.memset(gate_rows, 0.0)
@@ -184,11 +184,11 @@ def tile_list_rgg_ownP_kernel(
             return codes[:].bitcast(FP8X4), scales[:]
 
         nc.vector.tensor_copy(src_s[:], tab_s.indirect(src_list[:]))
-        for r in range(4):
-            nc.sync.dma_start(src_s1[r:P:32, :].bitcast(I32), src_s[4 + r : P : 32, :].bitcast(I32))
         nc.vector.tensor_copy(dst_s[:], tab_s.indirect(dst_list[:]))
         halves = [slice(h * N // 2, (h + 1) * N // 2) for h in range(2)]
         wo_raw = [[load_rows(wo, 0, "wo_raw00", halves[0])]]
+        for r in range(4):
+            nc.sync.dma_start(src_s1[r:P:32, :].bitcast(I32), src_s[4 + r : P : 32, :].bitcast(I32))
         tab_w.append(load_table(1))
         wo_raw[0].append(load_rows(wo, 0, "wo_raw01", halves[1]))
         wo_raw.append([load_rows(wo, 1, "wo_raw1%d" % h, halves[h], 2 - 2 * h) for h in range(2)])

@@ -65,7 +65,7 @@ def tile_list_rgg_ownP_kernel(
         places["gate_first"] = places["wa_raw1"] + 2 * KIB
         places["picked16"] = places["gate_first"]
         places["picked14s"] = places["gate_first"] + KIB
-        places["picked14"] = places["wo1_bf1"]
+        places["picked14"] = places["wo1_bf0"]
         places["page%d" % LAST_PAGE] = places["wa0_bf0"] + 6 * KIB
         for h in range(2):
             places["pairs%d" % h] = places["tab_w%d" % h]
@@ -186,10 +186,10 @@ def tile_list_rgg_ownP_kernel(
         nc.vector.tensor_copy(src_s[:], tab_s.indirect(src_list[:]))
         nc.vector.tensor_copy(dst_s[:], tab_s.indirect(dst_list[:]))
         halves = [slice(h * N // 2, (h + 1) * N // 2) for h in range(2)]
-        wo_raw = [[load_rows(wo, 0, "wo_raw00", halves[0])]]
         for r in range(4):
             nc.sync.dma_start(src_s1[r:P:32, :].bitcast(I32), src_s[4 + r : P : 32, :].bitcast(I32))
         tab_w.append(load_table(1))
+        wo_raw = [[load_rows(wo, 0, "wo_raw00", halves[0])]]
         wo_raw[0].append(load_rows(wo, 0, "wo_raw01", halves[1]))
         wo_raw.append([load_rows(wo, 1, "wo_raw1%d" % h, halves[h], 2 - 2 * h) for h in range(2)])
         wc_w = at_place("wc_w", [P, PASSES, N], U32)

from contextlib import ExitStack

import concourse.mybir as mybir
from concourse.masks import make_identity

K, N, T, J = 1024, 512, 2048, 1024
FLOPS = 2 * 4 * K * N * J

F32 = mybir.dt.float32
BF16 = mybir.dt.bfloat16
I32 = mybir.dt.int32
U32 = mybir.dt.uint32
U16 = mybir.dt.uint16
U8 = mybir.dt.uint8
FP8X4 = mybir.dt.float8_e4m3fn_x4
FP4X4 = mybir.dt.float4_e2m1fn_x4
MULT = mybir.AluOpType.mult
ADD = mybir.AluOpType.add
ACT = mybir.ActivationFunctionType

P = 128
PACK = 4
PASSES = K // (P * PACK)
TILES = J // P
PAIRS = TILES // 2
QUADS = 4
GROUP = 16
CHUNK = 512
CHUNKS = T // CHUNK
SRC, DST = 0, 1
KIB = 1024

PAGE_ORDER = (0, 2, 1, 3)
LAST_PAGE = PAGE_ORDER[-1]


def tile_list_rgg_ownP_kernel(
    tc, tab_words, tab_scales, wa, wb_words, wb_scales, wc_words, wc_scales, wo, wgo, offs, offs2, out_0, out_1, out_2
):
    nc = tc.nc
    with ExitStack() as ctx:
        lists = ctx.enter_context(tc.tile_pool(name="lists", bufs=1))
        keep = ctx.enter_context(tc.tile_pool(name="keep", bufs=1))
        staged = ctx.enter_context(tc.tile_pool(name="staged", bufs=1))
        psum = ctx.enter_context(tc.psum_pool(name="psum", bufs=1))

        def sb(name, shape, dtype, tag=None):
            return keep.tile(shape, dtype, name=name, tag=tag or name, align_bytes=64)

        first = [("wa_raw0", 8), ("wb_s", 2), ("gate_rows", 1)]
        second = [("tab_w0", 8), ("wa_raw1", 8), ("wc_s", 2), ("src_s1", 2)]
        cleared = [("page%d" % t, 8) for t in PAGE_ORDER[:3]] + [("src_s", 1), ("dst_s", 1)]
        after_scales = [("tab_s", 3), ("tab_w1", 8), ("wo_raw00", 4), ("wo_raw01", 4), ("wo_raw10", 6), ("wo_raw11", 4), ("wc_w", 4)]
        rounded = [("wa0_bf0", 14), ("wa1_bf0", 4), ("wo0_bf0", 2), ("wo0_bf1", 2), ("wo1_bf0", 2), ("wo1_bf1", 2), ("own0", 4), ("own1", 4)]
        placed = first + second + cleared + after_scales + rounded
        places = {name: KIB * sum(size for other, size in placed[:i]) for i, (name, unused) in enumerate(placed)}
        places["draft"] = places[cleared[0][0]]
        for k in range(2):
            places["eta%d" % k] = places["wo_raw10"] + 2 * KIB * k
            places["scaled%d" % (k + 2)] = places["own%d" % k] + 2 * KIB
        places["eta2"] = places["wo_raw10"] + 4 * KIB
        places["eta3"] = places["own1"]
        places["gate"] = places["wa_raw1"]
        places["picked02"] = places["wa0_bf0"]
        places["gate_first"] = places["wa_raw1"] + 2 * KIB
        places["picked16"] = places["gate_first"]
        places["picked14s"] = places["gate_first"] + KIB
        places["picked14"] = places["wo1_bf0"]
        places["page%d" % LAST_PAGE] = places["wa0_bf0"] + 6 * KIB
        for h in range(2):
            places["pairs%d" % h] = places["tab_w%d" % h]
        for c in range(CHUNKS):
            places["woven%d" % c] = places["wa_raw%d" % (c // 2)] + 4 * KIB * (c % 2)

        def at_place(name, shape, dtype):
            return staged.tile(shape, dtype, name=name, tag=name, align_bytes=64, offset=places[name])

        def bank(b, name):
            return psum.tile([P, N], F32, name=name, tag="bank%d" % b)

        src_list = lists.tile([P, J // GROUP], U16, name="src_list")
        dst_list = lists.tile([P, J // GROUP], U16, name="dst_list")
        nc.sync.dma_start(src_list[:], offs)
        nc.sync.dma_start(dst_list[:], offs2)
        both_lists = (src_list, dst_list)

        warm_in = sb("warm_in", [P, 1], F32)
        nc.gpsimd.memset(warm_in[:], 0.0)
        warm = sb("warm", [P, 1], F32)
        nc.scalar.activation(warm[:], warm_in[:], ACT.Sigmoid)

        def entries(lst, first, last):
            return lst[:, first * P // GROUP : last * P // GROUP]

        def region(name, parts, dtype, size):
            return at_place(name, [P, KIB * sum(kib for other, kib in parts) // size], dtype)

        def zeroed(tile, size):
            nc.vector.memset(tile[:, 0:size].bitcast(I32), 0)
            return tile[:, 0:size]

        draft = region("draft", cleared, F32, 4)[:, 0:P]
        make_identity(nc, draft)
        tab_s = zeroed(at_place("tab_s", [P, T], U8), T)
        wb_s = zeroed(at_place("wb_s", [P, J], U8), J).rearrange("p (a n) -> p a n", a=PASSES)
        gate_rows = at_place("gate_rows", [P, P], F32)[:]
        nc.vector.memset(gate_rows, 0.0)
        wc_s = zeroed(at_place("wc_s", [P, J], U8), J).rearrange("p (a n) -> p a n", a=PASSES)
        src_s1 = zeroed(at_place("src_s1", [P, J], U8), J)
        ident = sb("ident", [P, P], F32)
        nc.vector.tensor_copy(ident[:], draft)

        pages = {}

        def clear_page(t):
            pages[t] = at_place("page%d" % t, [P, T], F32)
            nc.gpsimd.memset(pages[t][:].bitcast(I32), 0)

        for t in PAGE_ORDER[:3]:
            clear_page(t)

        wb_w = sb("wb_w", [P, PASSES, 2 * N], U8)
        nc.sync.dma_start(wb_w[:].bitcast(I32), wb_words.rearrange("a p b -> p a b").bitcast(I32))
        for q in range(QUADS):
            nc.sync.dma_start(tab_s[32 * q : 32 * q + 8, :].bitcast(I32), tab_scales[:, 4 * q : 4 * q + 4, :].bitcast(I32))

        def load_scales(plane, scales):
            for r in range(4):
                nc.sync.dma_start(
                    plane[r:P:32, :, :].bitcast(I32), scales[:, r:16:4, :].rearrange("a q n -> q a n").bitcast(I32)
                )

        def load_rows(w, a, name, cols=slice(0, N), spare=0):
            raw = at_place(name, [P, PACK + spare, cols.stop - cols.start], F32)[:, 0:PACK, :]
            nc.sync.dma_start(raw, w[a * P * PACK : (a + 1) * P * PACK, cols].rearrange("(p i) n -> p i n", i=PACK))
            return raw

        def load_table(a):
            words = at_place("tab_w%d" % a, [P, T], I32)
            nc.sync.dma_start(words[:], tab_words[a].rearrange("p t i -> p (t i)").bitcast(I32))
            return words

        wa_raw = [load_rows(wa, 0, "wa_raw0")]
        load_scales(wb_s, wb_scales)
        nc.sync.dma_start(gate_rows[0:TILES, :], wgo[0:1, :].rearrange("o (b c) -> (o b) c", c=P))
        tab_w = [load_table(0)]
        load_scales(wc_s, wc_scales)
        wa_raw.append(load_rows(wa, 1, "wa_raw1"))

        src_s = at_place("src_s", [P, J], U8)
        dst_s = at_place("dst_s", [P, J], U8)

        gate_ps = bank(7, "gate_ps")
        nc.tensor.transpose(gate_ps[:, 0:P], gate_rows, ident[:])
        gate = at_place("gate", [P, TILES], F32)
        nc.scalar.copy(gate[:], gate_ps[:, 0:TILES])
        gate_first = at_place("gate_first", [P, N], F32)[:, 0:2]
        nc.scalar.copy(gate_first, gate_ps[:, 0:2])

        def gpsimd_round(out, in_):
            nc.gpsimd.tensor_scalar(out, in_, 1.0, -0.0, MULT, ADD)

        picked = {}

        def gather_words(a, first, last, sides=(DST, SRC), mark=""):
            name, shape = "picked%d%d%s" % (a, first, mark), [P, len(sides), (last - first) * P]
            words = (at_place if name in places else sb)(name, shape, U32)
            for i, s in enumerate(sides):
                nc.vector.tensor_copy(words[:, i, :], tab_w[a][:].bitcast(U32).indirect(entries(both_lists[s], first, last)))
                for k in range(first, last):
                    picked[a, k, s] = words[:, i, (k - first) * P : (k - first + 1) * P]

        def quantise_weight(raws, name, copies, spare=0):
            codes = sb(name + "_codes", [P, N], U32)
            scales = sb(name + "_scales", [P, N], U8)
            width = N // len(raws)
            for j, raw in enumerate(raws):
                cols = slice(j * width, (j + 1) * width)
                grouped = at_place("%s_bf%d" % (name, j), [P, width + spare * (1 - j), PACK], BF16)[:, 0:width, :]
                copies[j](grouped.rearrange("p (c e) i -> p c i e", e=4), raw.rearrange("p i (c e) -> p c i e", e=4))
                nc.vector.quantize_mx(
                    out=codes[:, cols].bitcast(FP8X4), scales=scales[:, cols], in_=grouped.rearrange("p n i -> p (n i)")
                )
            return codes[:].bitcast(FP8X4), scales[:]

        nc.vector.tensor_copy(src_s[:], tab_s.indirect(src_list[:]))
        nc.vector.tensor_copy(dst_s[:], tab_s.indirect(dst_list[:]))
        halves = [slice(h * N // 2, (h + 1) * N // 2) for h in range(2)]
        for r in range(4):
            nc.sync.dma_start(src_s1[r:P:32, :].bitcast(I32), src_s[4 + r : P : 32, :].bitcast(I32))
        tab_w.append(load_table(1))
        wo_raw = [[load_rows(wo, 0, "wo_raw00", halves[0])]]
        wo_raw[0].append(load_rows(wo, 0, "wo_raw01", halves[1]))
        wo_raw.append([load_rows(wo, 1, "wo_raw1%d" % h, halves[h], 2 - 2 * h) for h in range(2)])
        wc_w = at_place("wc_w", [P, PASSES, N], U32)
        nc.sync.dma_start(wc_w[:].bitcast(I32), wc_words.rearrange("a p n i -> p a (n i)").bitcast(I32))
        gather_words(0, 0, 2)
        wa_q = [quantise_weight([wa_raw[0]], "wa0", [nc.scalar.copy], N)]
        clear_page(LAST_PAGE)
        gather_words(0, 2, 8)
        wa_q.append(quantise_weight([wa_raw[1]], "wa1", [nc.scalar.copy]))
        gather_words(1, 0, 2)
        gather_words(1, 2, 4)
        wo_q = [quantise_weight(wo_raw[0], "wo0", [nc.scalar.copy, nc.scalar.copy])]
        wo_q.append(quantise_weight(wo_raw[1], "wo1", [nc.scalar.copy, nc.vector.tensor_copy]))
        gather_words(1, 4, 6, (DST,))
        wb_q = [(wb_w[:, a, :].bitcast(FP4X4), wb_s[:, a, :]) for a in range(PASSES)]
        wc_q = [(wc_w[:, a, :].bitcast(FP8X4), wc_s[:, a, :]) for a in range(PASSES)]

        def mx_pass(acc, k, s, a, weight, start, stop):
            cols = slice(k * P, (k + 1) * P)
            if weight is wb_q:
                plane = (src_s, src_s1)[a][:, cols]
            else:
                plane = (src_s, dst_s)[s][4 * a : P, cols]
            nc.tensor.matmul_mx(
                out=acc[:],
                lhsT=picked[a, k, s].bitcast(FP8X4),
                lhsT_scale=plane,
                rhs=weight[a][0],
                rhs_scale=weight[a][1],
                start=start,
                stop=stop,
            )

        def dealt(acc):
            return acc[:].rearrange("p (m t) -> p t m", t=PACK)

        msg, own, sums, etas, later = {}, {}, {}, {}, []

        def gating(k):
            za = bank(k if k < 4 else k % 2, "za%d" % k)
            for a in range(PASSES):
                mx_pass(za, k, DST, a, wa_q, a == 0, False)
                mx_pass(za, k, SRC, a, wb_q, False, a == PASSES - 1)
            eta = (at_place if k < 4 else sb)("eta%d" % k, [P, PACK, P], F32)
            nc.scalar.activation(eta[:], dealt(za), ACT.Sigmoid)
            etas[k] = eta

        def message(k):
            eta = etas[k]
            ms = bank(4 + k % 2, "ms%d" % k)
            for a in range(PASSES):
                mx_pass(ms, k, SRC, a, wc_q, a == 0, a == PASSES - 1)
            msg[k] = sb("msg%d" % k, [P, PACK, P], F32)
            if k < 2:
                even = slice(0, PACK, 2)
                nc.vector.scalar_tensor_tensor(
                    msg[k][:, even, :], dealt(ms)[:, even, :], gate_first[:, k : k + 1], eta[:, even, :], MULT, MULT
                )
                later.append((k, ms, eta))
            else:
                scaled = (at_place if k < 4 else sb)("scaled%d" % k, [P, PACK, P], F32)
                nc.scalar.activation(scaled[:], dealt(ms), ACT.Copy, scale=gate[:, k : k + 1])
                nc.gpsimd.tensor_tensor(msg[k][:], scaled[:], eta[:], MULT)

        def projection(k):
            ow = bank(6 + k if k < 2 else 2 + k % 2, "ow%d" % k)
            for a in range(PASSES):
                mx_pass(ow, k, DST, a, wo_q, a == 0, a == PASSES - 1)
            sums[k] = ow
            if k < 2:
                scale_own(k, 0, 2, at_place)
            else:
                scale_own(k, 0, 1, sb)

        def scale_own(k, first, step, make):
            part = make("own%d" % (k + TILES * first), [P, 2 * PACK if make is at_place else PACK // step, P], F32)
            part = part[:, 0 : PACK // step, :]
            nc.scalar.activation(part, dealt(sums[k])[:, first:PACK:step, :], ACT.Copy, scale=gate[:, k : k + 1])
            for t in range(first, PACK, step):
                own[k, t] = part[:, t // step, :]

        def place_results(b, pieces, tag=None):
            name = "%d%d" % pieces[0][0:2]
            acc = bank(b, "turn" + name)
            col = 0
            for t, first, last in pieces:
                for k in range(first, last):
                    cols = acc[:, col : col + P]
                    nc.tensor.matmul(cols, own[k, t], ident[:], start=True, stop=False, is_transpose=True)
                    nc.tensor.matmul(cols, msg[k][:, t, :], ident[:], start=False, stop=True, is_transpose=True)
                    col = col + P
            vals = sb("vals" + name, [P, col], F32, tag)
            nc.scalar.copy(vals[:], acc[:, 0:col])
            col = 0
            for t, first, last in pieces:
                width = (last - first) * P
                nc.vector.tensor_copy(pages[t][:].indirect(entries(dst_list, first, last)), vals[:, col : col + width])
                col = col + width

        def place_pair(g, u):
            two_pages = PAGE_ORDER[2 * u : 2 * u + 2]
            place_results(0 if g == 0 else 6 + u, [(t, 2 * g, 2 * g + 2) for t in two_pages if g < PAIRS // 2 or t != LAST_PAGE])

        for k in range(2):
            gating(k)
            message(k)
        gather_words(1, 4, 8, (SRC,), "s")
        gather_words(1, 6, 8, (DST,))
        for k in range(2):
            projection(k)
        for u in range(2):
            place_results(u, [(PAGE_ORDER[u], 0, 2)])
        for k, ms, eta in later:
            scaled = sb("scaled%d" % k, [P, PACK // 2, P], F32)
            nc.scalar.activation(scaled[:], dealt(ms)[:, 1:PACK:2, :], ACT.Copy, scale=gate[:, k : k + 1])
            nc.gpsimd.tensor_tensor(msg[k][:, 1:PACK:2, :], scaled[:], eta[:, 1:PACK:2, :], MULT)
        for k in range(2):
            scale_own(k, 1, 2, sb)
        place_pair(0, 1)
        for k in range(2, 4):
            gating(k)
            message(k)
        for k in range(2, 4):
            projection(k)
        for k in range(4, 6):
            gating(k)
        for g in range(1, PAIRS):
            ahead = range(2 * g + 2, min(2 * g + 4, TILES))
            place_pair(g, 0)
            for k in ahead:
                message(k)
            place_pair(g, 1)
            for k in ahead:
                projection(k)
            for k in range(2 * g + 4, min(2 * g + 6, TILES)):
                gating(k)
        place_results(4, [(LAST_PAGE, TILES // 2, TILES)])

        pairs = [at_place("pairs%d" % h, [P, 2, 2, CHUNK, 2], BF16) for h in range(2)]
        out_rows = out_0.rearrange("(p t) c -> p t c", t=PACK)

        def round_page(t, first, last, copy):
            values = pages[t][:, first * CHUNK : last * CHUNK].rearrange("p (b c) -> p b c", c=CHUNK)
            h = first // 2
            copy(pairs[h][:, first - 2 * h : last - 2 * h, t // 2, :, t % 2], values)

        for t in PAGE_ORDER:
            nc.sync.dma_start(out_rows[:, t, :], pages[t][:])
            if t < 2:
                round_page(t, 0, 2, gpsimd_round)
                round_page(t, 2, 3, gpsimd_round)
                round_page(t, 3, 4, nc.scalar.copy)
            elif t == 2:
                both = pages[t][:, 0 : T // 2].rearrange("p (b c) -> p b c", c=CHUNK).unsqueeze(3).to_broadcast([P, 2, CHUNK, 2])
                nc.scalar.copy(pairs[0][:, :, 1, :, :], both)
                round_page(t, 2, 4, nc.scalar.copy)
            else:
                for c in range(CHUNKS):
                    round_page(t, c, c + 1, nc.vector.tensor_copy if c < 2 else nc.scalar.copy)

        woven = [at_place("woven%d" % c, [P, CHUNK, 2], U32) for c in range(CHUNKS)]

        def weave(c, copy, word, cols):
            words = pairs[c // 2][:, c % 2, :, :, :].rearrange("p u c e -> p u (c e)").bitcast(word)
            copy(woven[c][:, cols, :].bitcast(word), words[:, :, cols].rearrange("p u c -> p c u"))

        pieces = [(c, slice(0, CHUNK)) for c in range(CHUNKS)]
        for c, cols in pieces:
            if c < CHUNKS // 2:
                weave(c, nc.vector.tensor_copy, I32, cols)
            else:
                weave(c, nc.scalar.copy, U32, cols)
        out_s = sb("out_s", [P, T], U8)
        out_words = out_1[0].rearrange("p t i -> p (t i)").bitcast(I32)
        for c, cols in pieces:
            place = slice(c * CHUNK + cols.start, c * CHUNK + cols.stop)
            codes = sb("out_w%d" % place.start, [P, cols.stop - cols.start], U32)
            nc.vector.quantize_mx(
                out=codes[:].bitcast(FP8X4),
                scales=out_s[:, place],
                in_=woven[c][:, cols, :].rearrange("p c u -> p (c u)").bitcast(BF16),
            )
            nc.sync.dma_start(out_words[:, place], codes[:].bitcast(I32))
        for r in range(4):
            queue = (nc.scalar, nc.sync)[r % 2]
            queue.dma_start(out_2[0, r:16:4, :].bitcast(I32), out_s[r:P:32, :].bitcast(I32))
